import numpy as np
import ml_dtypes


def mxq(x, axis, fmt="e4m3"):
    dtype, down = {"e4m3": (ml_dtypes.float8_e4m3fn, 7), "e5m2": (ml_dtypes.float8_e5m2, 14)}[fmt]
    v = np.moveaxis(np.asarray(x, np.float32).astype(ml_dtypes.bfloat16).astype(np.float64), axis, -1)
    blocks = v.reshape(v.shape[:-1] + (-1, 32))
    amax = np.abs(blocks).max(-1, keepdims=True)
    byte = np.maximum(np.where(amax > 0, np.frexp(amax)[1] - 1 + 127, 0) - down, 1)
    scale = np.exp2(byte - 127.0)
    codes = (blocks / scale).astype(np.float32).astype(dtype).astype(np.float64)
    return np.moveaxis((codes * scale).reshape(v.shape), -1, axis)


WIDE = False


def mx_kscale(k):
    if not WIDE:
        return np.ones(k)
    levels = np.array([10, -10, 5, -5, 0])
    if k % 512:
        return np.exp2(np.random.permutation(np.resize(levels, k // 32))).repeat(32)
    a = np.empty((k // 512, 16))
    for p in range(k // 512):
        a[p, :8] = np.random.permutation(np.resize(levels, 8))
        for g in range(8):
            far = levels[np.abs(levels - a[p, g]) >= 10]
            a[p, g + 8] = far[np.random.randint(len(far))]
    return np.exp2(a.ravel()).repeat(32)


def f64(x):
    return np.asarray(x).astype(np.float64)


def striped(idx):
    return np.tile(idx.reshape(-1, 16).T, (8, 1)).astype(np.uint16)


def unstriped(offs):
    return offs[:16].T.reshape(-1).astype(np.int64)


E2M1 = np.array([0.0, 0.5, 1.0, 1.5, 2.0, 3.0, 4.0, 6.0, -0.0, -0.5, -1.0, -1.5, -2.0, -3.0, -4.0, -6.0])


def pack_weight(w, fmt):
    k, n = w.shape
    w = f64(np.asarray(w, np.float32).astype(ml_dtypes.bfloat16)).reshape(k // 32, 32, n)
    amax = np.abs(w).max(1)
    if fmt == "e4m3":
        byte = np.frexp(amax)[1] - 1 + 127 - 7
    else:
        mant, ex = np.frexp(amax / 6.0)
        byte = np.where(mant > 0.5, ex, ex - 1) + 127
    byte = np.clip(np.where(amax > 0, byte, 1), 1, 254)
    scaled = (w * np.exp2(127.0 - byte)[:, None, :]).reshape(k, n).astype(np.float32)
    by_word = np.ascontiguousarray(scaled.reshape(k // 512, 128, 4, n).transpose(0, 1, 3, 2))
    if fmt == "e4m3":
        words = by_word.astype(ml_dtypes.float8_e4m3fn).view(np.uint8)
    else:
        c = by_word.astype(ml_dtypes.float4_e2m1fn).view(np.uint8) & 0xF
        words = (c[..., 0::2] | (c[..., 1::2] << 4)).reshape(k // 512, 128, 2 * n)
    return np.ascontiguousarray(words), np.ascontiguousarray(byte.astype(np.uint8).reshape(k // 512, 16, n))


def unpack_weight(words, scales, fmt):
    g, _, n = scales.shape
    words = np.ascontiguousarray(words).reshape(g, 128, n, -1)
    if fmt == "e4m3":
        vals = words.view(ml_dtypes.float8_e4m3fn).astype(np.float64)
    else:
        nib = np.empty((g, 128, n, 4), np.uint8)
        nib[..., 0::2] = words & 0xF
        nib[..., 1::2] = words >> 4
        vals = E2M1[nib]
    vals = vals * np.repeat(np.exp2(scales.astype(np.float64) - 127.0), 8, axis=1)[..., None]
    return vals.transpose(0, 1, 3, 2).reshape(g * 512, n)


def gelu(v):
    return 0.5 * v * (1.0 + np.tanh(np.sqrt(2.0 / np.pi) * (v + 0.044715 * v**3)))


K, T, S, P, H, N = 1024, 4096, 1024, 512, 1024, 512


def setup_inputs():
    n = np.random.standard_normal
    s = mx_kscale(K)[:, None]
    u = mx_kscale(H)[:, None]
    d = {}
    d["tab_words"], d["tab_scales"] = pack_weight(n((K, T)) * s, "e2m1")
    d["offs"] = striped(np.random.permutation(T)[:S])
    d["w1"] = (1.5 * n((K, H)) / K**0.5 / s * u.T).astype(np.float32)
    d["w2_words"], d["w2_scales"] = pack_weight(1.5 * n((K, H)) / K**0.5 / s, "e4m3")
    d["pos1"] = striped(np.random.permutation(S)[:P])
    d["pos2"] = striped(np.random.permutation(S)[:P])
    d["gain"] = np.exp(0.4 * n(H)).astype(np.float32)
    d["w4_words"], d["w4_scales"] = pack_weight(2.0 * n((H, N)) / H**0.5 / u, "e2m1")
    d["bias"] = (0.6 * n(N)).astype(np.float32)
    d["load"] = np.exp(0.4 * n((N, P))).astype(np.float32)
    return d


def reference(tab_words, tab_scales, offs, w1, w2_words, w2_scales, pos1, pos2,
              gain, w4_words, w4_scales, bias, load):
    v = unpack_weight(tab_words, tab_scales, "e2m1")[:, unstriped(offs)]
    w2 = unpack_weight(w2_words, w2_scales, "e4m3")
    w4 = unpack_weight(w4_words, w4_scales, "e2m1")
    a = mxq(f64(w1), 0, "e4m3").T @ v
    b = w2.T @ v
    h = a / (1.0 + np.abs(b))
    inlet = h[:, unstriped(pos1)]
    outlet = h[:, unstriped(pos2)]
    z = np.minimum(inlet, f64(gain)[:, None] * outlet)
    y = w4.T @ mxq(z, 0, "e4m3")
    return f64(load) * y + f64(bias)[:, None]

@@ -1,0 +1,276 @@
+from contextlib import ExitStack
+
+import concourse.mybir as mybir
+
+K, T, S, PAIRS, H, N = 1024, 4096, 1024, 512, 1024, 512
+FLOPS = 2 * (2 * K * H * S + H * N * PAIRS)
+
+F32 = mybir.dt.float32
+BF16 = mybir.dt.bfloat16
+I32 = mybir.dt.int32
+U32 = mybir.dt.uint32
+U16 = mybir.dt.uint16
+U8 = mybir.dt.uint8
+FP8X4 = mybir.dt.float8_e4m3fn_x4
+FP4X4 = mybir.dt.float4_e2m1fn_x4
+ALU = mybir.AluOpType
+ACT = mybir.ActivationFunctionType
+
+P = 128
+PACK = 4
+PASS = P * PACK
+BANK = 512
+
+
+def tile_list_electrolyser_pair_minimum_kernel(
+    tc, tab_words, tab_scales, offs, w1, w2_words, w2_scales, pos1, pos2, gain, w4_words, w4_scales, bias, load, out
+):
+    nc = tc.nc
+    with ExitStack() as ctx:
+        held = ctx.enter_context(tc.tile_pool(name="held", bufs=1))
+        big = ctx.enter_context(tc.tile_pool(name="big", bufs=1))
+        ring = ctx.enter_context(tc.tile_pool(name="ring", bufs=2))
+        psum = ctx.enter_context(tc.psum_pool(name="psum", bufs=4))
+
+        offs_sb = held.tile([P, S // 16], U16, name="offs_sb")
+        pos1_sb = held.tile([P, PAIRS // 16], U16, name="pos1_sb")
+        pos2_sb = held.tile([P, PAIRS // 16], U16, name="pos2_sb")
+
+        tab_bytes = big.tile([P, T], U8, name="tab_bytes", tag="tab_bytes", align_bytes=64)
+        v_plane = held.tile([P, 2, S], U8, name="v_plane", align_bytes=64)
+        w2_planes = held.tile([P, 2, H], U8, name="w2_planes", align_bytes=64)
+        warm = held.tile([P, 2], F32, name="warm")
+        nc.vector.memset(warm[:, 0:1], 1.0)
+        nc.scalar.activation(warm[:, 1:2], warm[:, 0:1], ACT.Abs_reciprocal_sqrt)
+
+        def load_planes(engine, planes, scales):
+            nc.vector.memset(planes[:].rearrange("p a c -> p (a c)").bitcast(I32), 0)
+            for q in range(4):
+                engine.dma_start(
+                    out=planes[32 * q : 32 * q + 4, :, :].bitcast(I32),
+                    in_=scales[:, 4 * q : 4 * q + 4, :].rearrange("a r c -> r a c").bitcast(I32),
+                )
+
+        def load_table(a):
+            words = big.tile([P, T], U16, name="tab_w", tag="tab%d" % a, align_bytes=64)
+            nc.sync.dma_start(out=words[:].bitcast(I32), in_=tab_words[a].bitcast(I32))
+            return words
+
+        def load_w1(g, a, c0, c1, tag="w1raw"):
+            raw = big.tile([P, PACK, c1 - c0], F32, name="w1_raw", tag=tag, align_bytes=64)
+            rows = w1[a * PASS : (a + 1) * PASS, g * PASS + c0 : g * PASS + c1]
+            nc.sync.dma_start(out=raw[:], in_=rows.rearrange("(p j) c -> p j c", j=PACK))
+            return raw
+
+        def load_w2(g):
+            raw = big.tile([P, 2, PASS], I32, name="w2_raw", tag="tab_bytes", align_bytes=64)
+            src = w2_words[:, :, g * PASS : (g + 1) * PASS, :].rearrange("a p c i -> p a (c i)")
+            nc.sync.dma_start(out=raw[:], in_=src.bitcast(I32))
+            return raw
+
+        def round_w1(copy, grouped, raw, c0, c1):
+            dst = grouped[:].rearrange("p (t m j) -> p m j t", t=PACK, j=PACK)[:, c0 // PACK : c1 // PACK]
+            copy(out=dst, in_=raw[:].rearrange("p j (m t) -> p m j t", t=PACK))
+
+        def quantize(grouped, name):
+            codes = held.tile([P, PASS], U32, name=name + "_codes", align_bytes=64)
+            plane = held.tile([P, PASS], U8, name=name + "_plane", align_bytes=64)
+            nc.vector.quantize_mx(out=codes[:].bitcast(FP8X4), scales=plane[:], in_=grouped[:])
+            return codes, plane
+
+        def deal_w2_words(g, raw):
+            dealt = held.tile([P, 2, PASS], I32, name="w2_dealt%d" % g, align_bytes=64)
+            nc.vector.tensor_copy(
+                out=dealt[:].rearrange("p a (t c i) -> p a c t i", t=PACK, i=4),
+                in_=raw[:].rearrange("p a (c i t) -> p a c t i", t=PACK, i=4),
+            )
+            return dealt
+
+        def deal_w2_planes(g):
+            dealt = held.tile([P, 2, PASS], U8, name="w2_plane_dealt%d" % g, align_bytes=64)
+            nc.vector.tensor_copy(
+                out=dealt[:].rearrange("p a (t m) -> p a m t", t=PACK),
+                in_=w2_planes[:, :, g * PASS : (g + 1) * PASS].rearrange("p a (m t) -> p a m t", t=PACK),
+            )
+            return dealt
+
+        v_words, v_planes = {}, {}
+
+        def gather_table(words, a, half):
+            cols = offs_sb[:, half * BANK // 16 : (half + 1) * BANK // 16]
+            picked = held.tile([P, BANK], U16, name="v_words%d%d" % (a, half), align_bytes=64)
+            nc.vector.tensor_copy(out=picked[:], in_=words[:].indirect(cols))
+            v_words[a, half], v_planes[a, half] = picked, v_plane[:, a, half * BANK : (half + 1) * BANK]
+
+        def first_product(tag, operands, t, half):
+            acc = psum.tile([P, BANK], F32, name="acc", tag=tag)
+            for a in range(2):
+                codes, plane = operands[a]
+                nc.tensor.matmul_mx(
+                    out=acc[:],
+                    lhsT=codes[:, t * P : (t + 1) * P].bitcast(FP8X4),
+                    lhsT_scale=plane[:, t * P : (t + 1) * P],
+                    rhs=v_words[a, half][:].bitcast(FP4X4),
+                    rhs_scale=v_planes[a, half],
+                    start=(a == 0),
+                    stop=(a == 1),
+                )
+            return acc
+
+        w1_q, w2_q = {}, {}
+
+        def damping(i, spans):
+            g, t = divmod(i, PACK)
+            size = ring.tile([P, S], F32, name="size")
+            root = ring.tile([P, S], F32, name="root")
+            damp = ring.tile([P, S], F32, name="damp", bufs=3)
+            for span in spans:
+                for half in span:
+                    b = first_product("b", w2_q[g], t, half)
+                    nc.scalar.activation(size[:, half * BANK : (half + 1) * BANK], b[:], ACT.Abs)
+                cols = slice(span[0] * BANK, (span[-1] + 1) * BANK)
+                nc.scalar.activation(root[:, cols], size[:, cols], ACT.Abs_reciprocal_sqrt, bias=1.0)
+                nc.scalar.activation(damp[:, cols], root[:, cols], ACT.Square)
+            return damp
+
+        def features(i, damp):
+            g, t = divmod(i, PACK)
+            h = ring.tile([P, S], F32, name="h")
+            for half in range(2):
+                cols = slice(half * BANK, (half + 1) * BANK)
+                a_sum = first_product("a", w1_q[g], t, half)
+                nc.vector.tensor_tensor(h[:, cols], a_sum[:], damp[:, cols], ALU.mult)
+            return h
+
+        def pick(h):
+            inlet = ring.tile([P, PAIRS], F32, name="inlet")
+            outlet = ring.tile([P, PAIRS], F32, name="outlet")
+            nc.vector.tensor_copy(out=inlet[:], in_=h[:].indirect(pos1_sb[:]))
+            nc.vector.tensor_copy(out=outlet[:], in_=h[:].indirect(pos2_sb[:]))
+            return inlet, outlet
+
+        def lower(i, z_rows, picked):
+            inlet, outlet = picked
+            nc.vector.scalar_tensor_tensor(
+                out=z_rows[:, i % PACK, :], in0=outlet[:], scalar=gain_sb[:, i : i + 1], in1=inlet[:],
+                op0=ALU.mult, op1=ALU.min,
+            )
+
+        def weave_z(copy, grouped, z_rows, m0, m1):
+            copy(
+                out=grouped[:, m0 * PACK : m1 * PACK].rearrange("p (c i t) -> p c t i", t=PACK, i=4),
+                in_=z_rows[:, :, m0:m1].rearrange("p t (c i) -> p c t i", i=4),
+            )
+
+        nc.sync.dma_start(
+            out=tab_bytes[96:128, :].bitcast(I32), in_=tab_scales.rearrange("a q c -> (a q) c").bitcast(I32)
+        )
+        nc.sync.dma_start(offs_sb[:], offs)
+        nc.vector.memset(tab_bytes[0:96, :].bitcast(I32), 0)
+        load_planes(nc.gpsimd, w2_planes, w2_scales)
+        nc.vector.memset(v_plane[:].rearrange("p a c -> p (a c)").bitcast(I32), 0)
+        tab0 = load_table(0)
+        raw00 = load_w1(0, 0, 0, PASS)
+        tab1 = load_table(1)
+        nc.sync.dma_start(pos1_sb[:], pos1)
+        nc.sync.dma_start(pos2_sb[:], pos2)
+
+        v_bytes = held.tile([P, S], U8, name="v_bytes", align_bytes=64)
+        nc.vector.tensor_copy(out=v_bytes[:], in_=tab_bytes[:].indirect(offs_sb[:]))
+        for a in range(2):
+            for q in range(4):
+                row = 96 + 16 * a + 4 * q
+                nc.scalar.dma_start(
+                    out=v_plane[32 * q : 32 * q + 4, a, :].bitcast(I32), in_=v_bytes[row : row + 4, :].bitcast(I32)
+                )
+        w2raw = load_w2(0)
+
+        gather_table(tab0, 0, 0)
+        gather_table(tab0, 0, 1)
+        raw01 = [load_w1(0, 1, 0, 256, "tab0"), load_w1(0, 1, 256, PASS, "w1late")]
+        grouped00 = ring.tile([P, PASS * PACK], BF16, name="grouped", align_bytes=64)
+        round_w1(nc.scalar.copy, grouped00, raw00, 0, PASS)
+        planes0 = deal_w2_planes(0)
+        gather_table(tab1, 1, 0)
+        words0 = deal_w2_words(0, w2raw)
+        w2_q[0] = [(words0[:, a, :], planes0[:, a, :]) for a in range(2)]
+        gather_table(tab1, 1, 1)
+        gain_sb = big.tile([P, 2 * PACK], F32, name="gain_sb", tag="tab1", align_bytes=64)
+        with nc.allow_non_contiguous_dma("small vectors onto the partitions"):
+            nc.sync.dma_start(
+                out=gain_sb[:].rearrange("p (g t) -> p g t", t=PACK),
+                in_=gain.rearrange("(g p t) -> p g t", p=P, t=PACK),
+            )
+        q00 = quantize(grouped00, "w1q00")
+        damps = {0: damping(0, [(0,), (1,)])}
+        grouped01 = ring.tile([P, PASS * PACK], BF16, name="grouped", align_bytes=64)
+        round_w1(nc.vector.tensor_copy, grouped01, raw01[0], 0, 256)
+        round_w1(nc.vector.tensor_copy, grouped01, raw01[1], 256, PASS)
+        w1_q[0] = [q00, quantize(grouped01, "w1q01")]
+
+        w2raw1 = load_w2(1)
+        raw10 = load_w1(1, 0, 0, PASS)
+        raw11 = [load_w1(1, 1, 0, 256, "tab0"), load_w1(1, 1, 256, PASS, "w1late")]
+
+        z_rows = [held.tile([P, PACK, PAIRS], BF16, name="z_rows%d" % g) for g in range(2)]
+        z_q = []
+        picked = None
+        for i in range(2 * PACK):
+            if i + 1 < 2 * PACK:
+                damps[i + 1] = damping(i + 1, [(0, 1)])
+            h = features(i, damps[i])
+            if i > 0:
+                lower(i - 1, z_rows[(i - 1) // PACK], picked)
+            picked = pick(h)
+            if i == 0:
+                planes1 = deal_w2_planes(1)
+                words1 = deal_w2_words(1, w2raw1)
+                w2_q[1] = [(words1[:, a, :], planes1[:, a, :]) for a in range(2)]
+                grouped10 = ring.tile([P, PASS * PACK], BF16, name="grouped", align_bytes=64)
+                round_w1(nc.scalar.copy, grouped10, raw10, 0, PASS)
+            if i == 1:
+                q10 = quantize(grouped10, "w1q10")
+                grouped11 = ring.tile([P, PASS * PACK], BF16, name="grouped", align_bytes=64)
+                round_w1(nc.scalar.copy, grouped11, raw11[0], 0, 256)
+                round_w1(nc.scalar.copy, grouped11, raw11[1], 256, PASS)
+            if i == 2:
+                w1_q[1] = [q10, quantize(grouped11, "w1q11")]
+                load_sb = big.tile([P, N // P, PAIRS], F32, name="load_sb", tag="w1raw", align_bytes=64)
+                nc.sync.dma_start(out=load_sb[:], in_=load.rearrange("(c p) m -> p c m", p=P))
+                w4_sb = big.tile([P, 2, N], U16, name="w4_sb", tag="tab0", align_bytes=64)
+                nc.sync.dma_start(out=w4_sb[:].bitcast(I32), in_=w4_words.rearrange("a p c -> p a c").bitcast(I32))
+                w4_planes = big.tile([P, 2, N], U8, name="w4_planes", tag="tab_bytes", align_bytes=64)
+                load_planes(nc.sync, w4_planes, w4_scales)
+                bias_sb = big.tile([P, N // P], F32, name="bias_sb", tag="w1late", align_bytes=64)
+                with nc.allow_non_contiguous_dma("one bias value to a partition"):
+                    nc.sync.dma_start(out=bias_sb[:], in_=bias.rearrange("(c p) -> p c", p=P))
+            if i == PACK:
+                z_grouped0 = ring.tile([P, PAIRS * PACK], BF16, name="grouped", align_bytes=64)
+                weave_z(nc.scalar.copy, z_grouped0, z_rows[0], 0, PAIRS)
+            if i == PACK + 1:
+                z_q.append(quantize(z_grouped0, "zq0"))
+        lower(2 * PACK - 1, z_rows[1], picked)
+        z_grouped1 = ring.tile([P, PAIRS * PACK], BF16, name="grouped", align_bytes=64)
+        weave_z(nc.scalar.copy, z_grouped1, z_rows[1], 0, 192)
+        weave_z(nc.vector.tensor_copy, z_grouped1, z_rows[1], 192, PAIRS)
+        z_q.append(quantize(z_grouped1, "zq1"))
+
+        ys = [psum.tile([P, BANK], F32, name="y", tag="b") for c in range(N // P)]
+        for g in range(2):
+            for c in range(N // P):
+                codes, plane = z_q[g]
+                nc.tensor.matmul_mx(
+                    out=ys[c][:],
+                    lhsT=w4_sb[:, g, c * P : (c + 1) * P].bitcast(FP4X4),
+                    lhsT_scale=w4_planes[:, g, c * P : (c + 1) * P],
+                    rhs=codes[:].bitcast(FP8X4),
+                    rhs_scale=plane[:],
+                    start=(g == 0),
+                    stop=(g == 1),
+                )
+        for c in range(N // P):
+            weighted = ring.tile([P, PAIRS], F32, name="weighted", bufs=4)
+            score = ring.tile([P, PAIRS], F32, name="score", bufs=4)
+            nc.vector.tensor_tensor(weighted[:], ys[c][:], load_sb[:, c, :], ALU.mult)
+            nc.scalar.activation(score[:], weighted[:], ACT.Identity, bias=bias_sb[:, c : c + 1])
+            nc.sync.dma_start(out=out[c * P : (c + 1) * P, :], in_=score[:])

@@ -37,45 +37,43 @@ def tile_list_electrolyser_pair_minimum_kernel(
         pos2_sb = held.tile([P, PAIRS // 16], U16, name="pos2_sb")
 
         tab_bytes = big.tile([P, T], U8, name="tab_bytes", tag="tab_bytes", align_bytes=64)
-        v_plane = held.tile([P, 2, S], U8, name="v_plane", align_bytes=64)
-        w2_planes = held.tile([P, 2, H], U8, name="w2_planes", align_bytes=64)
+        w2_bytes = big.tile([P, H], U8, name="w2_bytes", tag="w2_bytes", align_bytes=64)
+        planes = [held.tile([P, S + H], U8, name="planes%d" % a, align_bytes=64) for a in range(2)]
         warm = held.tile([P, 2], F32, name="warm")
         nc.vector.memset(warm[:, 0:1], 1.0)
         nc.scalar.activation(warm[:, 1:2], warm[:, 0:1], ACT.Abs_reciprocal_sqrt)
 
-        def load_planes(engine, planes, scales):
-            nc.vector.memset(planes[:].rearrange("p a c -> p (a c)").bitcast(I32), 0)
-            for q in range(4):
-                engine.dma_start(
-                    out=planes[32 * q : 32 * q + 4, :, :].bitcast(I32),
-                    in_=scales[:, 4 * q : 4 * q + 4, :].rearrange("a r c -> r a c").bitcast(I32),
-                )
+        def load_scale_rows(dst, scales):
+            nc.sync.dma_start(out=dst.bitcast(I32), in_=scales.rearrange("a q c -> (a q) c").bitcast(I32))
 
         def load_table(a):
             words = big.tile([P, T], U16, name="tab_w", tag="tab%d" % a, align_bytes=64)
             nc.sync.dma_start(out=words[:].bitcast(I32), in_=tab_words[a].bitcast(I32))
             return words
 
-        def load_w1(g, a, c0, c1, tag="w1raw"):
+        def load_w1(g, a, c0, c1, tag):
             raw = big.tile([P, PACK, c1 - c0], F32, name="w1_raw", tag=tag, align_bytes=64)
             rows = w1[a * PASS : (a + 1) * PASS, g * PASS + c0 : g * PASS + c1]
             nc.sync.dma_start(out=raw[:], in_=rows.rearrange("(p j) c -> p j c", j=PACK))
             return raw
 
         def load_w2(g):
-            raw = big.tile([P, 2, PASS], I32, name="w2_raw", tag="tab_bytes", align_bytes=64)
+            raw = big.tile([P, 2, PASS], I32, name="w2_raw", tag="w2raw", align_bytes=64)
             src = w2_words[:, :, g * PASS : (g + 1) * PASS, :].rearrange("a p c i -> p a (c i)")
             nc.sync.dma_start(out=raw[:], in_=src.bitcast(I32))
             return raw
 
         def round_w1(copy, grouped, raw, c0, c1):
-            dst = grouped[:].rearrange("p (t m j) -> p m j t", t=PACK, j=PACK)[:, c0 // PACK : c1 // PACK]
+            dst = grouped.rearrange("p (t m j) -> p m j t", t=PACK, j=PACK)[:, c0 // PACK : c1 // PACK]
             copy(out=dst, in_=raw[:].rearrange("p j (m t) -> p m j t", t=PACK))
 
-        def quantize(grouped, name):
-            codes = held.tile([P, PASS], U32, name=name + "_codes", align_bytes=64)
-            plane = held.tile([P, PASS], U8, name=name + "_plane", align_bytes=64)
-            nc.vector.quantize_mx(out=codes[:].bitcast(FP8X4), scales=plane[:], in_=grouped[:])
+        def quantize(grouped, name, cuts=(0, PASS)):
+            codes = held.tile([P, cuts[-1]], U32, name=name + "_codes", align_bytes=64)
+            plane = held.tile([P, cuts[-1]], U8, name=name + "_plane", align_bytes=64)
+            for c0, c1 in zip(cuts, cuts[1:]):
+                nc.vector.quantize_mx(
+                    out=codes[:, c0:c1].bitcast(FP8X4), scales=plane[:, c0:c1], in_=grouped[:, c0 * PACK : c1 * PACK]
+                )
             return codes, plane
 
         def deal_w2_words(g, raw):
@@ -86,48 +84,46 @@ def tile_list_electrolyser_pair_minimum_kernel(
             )
             return dealt
 
-        def deal_w2_planes(g):
-            dealt = held.tile([P, 2, PASS], U8, name="w2_plane_dealt%d" % g, align_bytes=64)
-            nc.vector.tensor_copy(
-                out=dealt[:].rearrange("p a (t m) -> p a m t", t=PACK),
-                in_=w2_planes[:, :, g * PASS : (g + 1) * PASS].rearrange("p a (m t) -> p a m t", t=PACK),
-            )
-            return dealt
-
         v_words, v_planes = {}, {}
 
         def gather_table(words, a, half):
             cols = offs_sb[:, half * BANK // 16 : (half + 1) * BANK // 16]
             picked = held.tile([P, BANK], U16, name="v_words%d%d" % (a, half), align_bytes=64)
             nc.vector.tensor_copy(out=picked[:], in_=words[:].indirect(cols))
-            v_words[a, half], v_planes[a, half] = picked, v_plane[:, a, half * BANK : (half + 1) * BANK]
+            v_words[a, half], v_planes[a, half] = picked, planes[a][:, half * BANK : (half + 1) * BANK]
 
-        def first_product(tag, operands, t, half):
-            acc = psum.tile([P, BANK], F32, name="acc", tag=tag)
-            for a in range(2):
+        def first_product(tag, operands, t, passes):
+            accs = [psum.tile([P, BANK], F32, name="acc", tag=tag) for half in range(2)]
+            for a in passes:
                 codes, plane = operands[a]
-                nc.tensor.matmul_mx(
-                    out=acc[:],
-                    lhsT=codes[:, t * P : (t + 1) * P].bitcast(FP8X4),
-                    lhsT_scale=plane[:, t * P : (t + 1) * P],
-                    rhs=v_words[a, half][:].bitcast(FP4X4),
-                    rhs_scale=v_planes[a, half],
-                    start=(a == 0),
-                    stop=(a == 1),
-                )
-            return acc
+                for half in range(2):
+                    nc.tensor.matmul_mx(
+                        out=accs[half][:],
+                        lhsT=codes[:, t * P : (t + 1) * P].bitcast(FP8X4),
+                        lhsT_scale=plane[:, t * P : (t + 1) * P],
+                        rhs=v_words[a, half][:].bitcast(FP4X4),
+                        rhs_scale=v_planes[a, half],
+                        start=(a == passes[0]),
+                        stop=(a == passes[1]),
+                    )
+            return accs
 
         w1_q, w2_q = {}, {}
+        damp_all = held.tile([P, (2 * PACK + 1) * S], F32, name="damp_all")
+        root_tags = {2: "root_then_w1", 2 * PACK - 1: "root_then_z"}
 
         def damping(i, spans):
             g, t = divmod(i, PACK)
             size = ring.tile([P, S], F32, name="size")
-            root = ring.tile([P, S], F32, name="root")
-            damp = ring.tile([P, S], F32, name="damp", bufs=3)
+            if i in root_tags:
+                root = big.tile([P, S], F32, name="root", tag=root_tags[i], align_bytes=64)
+            else:
+                root = ring.tile([P, S], F32, name="root")
+            damp = damp_all[:, i * S : (i + 1) * S]
+            b = first_product("b", w2_q[g], t, (0, 1))
             for span in spans:
                 for half in span:
-                    b = first_product("b", w2_q[g], t, half)
-                    nc.scalar.activation(size[:, half * BANK : (half + 1) * BANK], b[:], ACT.Abs)
+                    nc.scalar.activation(size[:, half * BANK : (half + 1) * BANK], b[half][:], ACT.Abs)
                 cols = slice(span[0] * BANK, (span[-1] + 1) * BANK)
                 nc.scalar.activation(root[:, cols], size[:, cols], ACT.Abs_reciprocal_sqrt, bias=1.0)
                 nc.scalar.activation(damp[:, cols], root[:, cols], ACT.Square)
@@ -136,141 +132,174 @@ def tile_list_electrolyser_pair_minimum_kernel(
         def features(i, damp):
             g, t = divmod(i, PACK)
             h = ring.tile([P, S], F32, name="h")
+            a_sum = first_product("a", w1_q[g], t, (1 - g, g))
             for half in range(2):
                 cols = slice(half * BANK, (half + 1) * BANK)
-                a_sum = first_product("a", w1_q[g], t, half)
-                nc.vector.tensor_tensor(h[:, cols], a_sum[:], damp[:, cols], ALU.mult)
+                nc.vector.tensor_tensor(h[:, cols], a_sum[half][:], damp[:, cols], ALU.mult)
             return h
 
-        def pick(h):
-            inlet = ring.tile([P, PAIRS], F32, name="inlet")
-            outlet = ring.tile([P, PAIRS], F32, name="outlet")
-            nc.vector.tensor_copy(out=inlet[:], in_=h[:].indirect(pos1_sb[:]))
-            nc.vector.tensor_copy(out=outlet[:], in_=h[:].indirect(pos2_sb[:]))
-            return inlet, outlet
+        def pick(h, pos_sb, name, m0, m1):
+            picked = ring.tile([P, m1 - m0], F32, name="picked", tag=name, bufs=4)
+            nc.vector.tensor_copy(out=picked[:], in_=h[:].indirect(pos_sb[:, m0 // 16 : m1 // 16]))
+            return picked
 
-        def lower(i, z_rows, picked):
-            inlet, outlet = picked
+        def lower(i, inlet, outlet, m0, m1):
             nc.vector.scalar_tensor_tensor(
-                out=z_rows[:, i % PACK, :], in0=outlet[:], scalar=gain_sb[:, i : i + 1], in1=inlet[:],
+                out=damp_all[:, (i + 1) * S + m0 : (i + 1) * S + m1], in0=outlet[:], scalar=gain_sb[:, i : i + 1], in1=inlet[:],
                 op0=ALU.mult, op1=ALU.min,
             )
 
-        def weave_z(copy, grouped, z_rows, m0, m1):
+        def weave_z(copy, g, m0, m1, tag):
+            grouped = big.tile([P, (m1 - m0) * PACK], BF16, name="grouped", tag=tag, align_bytes=64)
+            z_rows = damp_all[:, (g * PACK + 1) * S : (g * PACK + PACK + 1) * S].rearrange("p (t s) -> p t s", t=PACK)
             copy(
-                out=grouped[:, m0 * PACK : m1 * PACK].rearrange("p (c i t) -> p c t i", t=PACK, i=4),
+                out=grouped[:].rearrange("p (c i t) -> p c t i", t=PACK, i=4),
                 in_=z_rows[:, :, m0:m1].rearrange("p t (c i) -> p c t i", i=4),
             )
+            return grouped
 
-        nc.sync.dma_start(
-            out=tab_bytes[96:128, :].bitcast(I32), in_=tab_scales.rearrange("a q c -> (a q) c").bitcast(I32)
-        )
+        half_cols = PASS // 2
         nc.sync.dma_start(offs_sb[:], offs)
-        nc.vector.memset(tab_bytes[0:96, :].bitcast(I32), 0)
-        load_planes(nc.gpsimd, w2_planes, w2_scales)
-        nc.vector.memset(v_plane[:].rearrange("p a c -> p (a c)").bitcast(I32), 0)
+        load_scale_rows(tab_bytes[0:32, :], tab_scales)
+        load_scale_rows(w2_bytes[0:32, :], w2_scales)
+        for rows in (slice(32, 64), slice(64, 128)):
+            nc.vector.memset(tab_bytes[rows, :].bitcast(I32), 0)
+            nc.vector.memset(w2_bytes[rows, :].bitcast(I32), 0)
+        nc.vector.memset(planes[1][:].bitcast(I32), 0)
         tab0 = load_table(0)
-        raw00 = load_w1(0, 0, 0, PASS)
-        tab1 = load_table(1)
         nc.sync.dma_start(pos1_sb[:], pos1)
         nc.sync.dma_start(pos2_sb[:], pos2)
-
-        v_bytes = held.tile([P, S], U8, name="v_bytes", align_bytes=64)
-        nc.vector.tensor_copy(out=v_bytes[:], in_=tab_bytes[:].indirect(offs_sb[:]))
-        for a in range(2):
-            for q in range(4):
-                row = 96 + 16 * a + 4 * q
-                nc.scalar.dma_start(
-                    out=v_plane[32 * q : 32 * q + 4, a, :].bitcast(I32), in_=v_bytes[row : row + 4, :].bitcast(I32)
-                )
-        w2raw = load_w2(0)
-
-        gather_table(tab0, 0, 0)
-        gather_table(tab0, 0, 1)
-        raw01 = [load_w1(0, 1, 0, 256, "tab0"), load_w1(0, 1, 256, PASS, "w1late")]
-        grouped00 = ring.tile([P, PASS * PACK], BF16, name="grouped", align_bytes=64)
-        round_w1(nc.scalar.copy, grouped00, raw00, 0, PASS)
-        planes0 = deal_w2_planes(0)
-        gather_table(tab1, 1, 0)
-        words0 = deal_w2_words(0, w2raw)
-        w2_q[0] = [(words0[:, a, :], planes0[:, a, :]) for a in range(2)]
-        gather_table(tab1, 1, 1)
-        gain_sb = big.tile([P, 2 * PACK], F32, name="gain_sb", tag="tab1", align_bytes=64)
-        with nc.allow_non_contiguous_dma("small vectors onto the partitions"):
+        gain_sb = held.tile([P, 2 * PACK], F32, name="gain_sb")
+        with nc.allow_non_contiguous_dma("four gains to a partition and group"):
             nc.sync.dma_start(
                 out=gain_sb[:].rearrange("p (g t) -> p g t", t=PACK),
                 in_=gain.rearrange("(g p t) -> p g t", p=P, t=PACK),
             )
-        q00 = quantize(grouped00, "w1q00")
+        w2raw = load_w2(0)
+        raw00a = load_w1(0, 0, 0, half_cols, "w1raw")
+        tab1 = load_table(1)
+
+        v_bytes = big.tile([P, S], U8, name="v_bytes", tag="v_bytes", align_bytes=64)
+        nc.vector.tensor_copy(out=v_bytes[:], in_=tab_bytes[:].indirect(offs_sb[:]))
+        nc.vector.tensor_copy(
+            out=planes[0][:, S : S + H].rearrange("p (g t m) -> p g m t", g=2, t=PACK),
+            in_=w2_bytes[:].rearrange("p (g m t) -> p g m t", g=2, t=PACK),
+        )
+        nc.vector.tensor_copy(out=planes[0][:, 0:S].bitcast(I32), in_=v_bytes[:].bitcast(I32))
+        for a in range(2):
+            for q in range(1 - a, 4):
+                row = 16 * a + 4 * q
+                queue = nc.gpsimd if (a, q) == (1, 3) else nc.sync
+                queue.dma_start(
+                    out=planes[a][32 * q : 32 * q + 4, :].bitcast(I32), in_=planes[0][row : row + 4, :].bitcast(I32)
+                )
+        raw01 = load_w1(0, 1, 0, PASS, "v_bytes")
+
+        gather_table(tab0, 0, 0)
+        gather_table(tab0, 0, 1)
+        raw00b = load_w1(0, 0, half_cols, PASS, "tab0")
+        grouped00 = ring.tile([P, PASS * PACK], BF16, name="grouped", align_bytes=64)
+        round_w1(nc.scalar.copy, grouped00[:], raw00a, 0, half_cols)
+        words0 = deal_w2_words(0, w2raw)
+        w2_q[0] = [(words0[:, a, :], planes[a][:, S : S + PASS]) for a in range(2)]
+        w2raw1 = load_w2(1)
+        gather_table(tab1, 1, 0)
+        gather_table(tab1, 1, 1)
+        raw10 = load_w1(1, 0, 0, PASS, "tab1")
         damps = {0: damping(0, [(0,), (1,)])}
         grouped01 = ring.tile([P, PASS * PACK], BF16, name="grouped", align_bytes=64)
-        round_w1(nc.vector.tensor_copy, grouped01, raw01[0], 0, 256)
-        round_w1(nc.vector.tensor_copy, grouped01, raw01[1], 256, PASS)
-        w1_q[0] = [q00, quantize(grouped01, "w1q01")]
+        round_w1(nc.vector.tensor_copy, grouped01[:], raw01, 0, PASS)
+        raw11 = load_w1(1, 1, 0, PASS, "v_bytes")
+        round_w1(nc.vector.tensor_copy, grouped00[:], raw00b, half_cols, PASS)
+        q01 = quantize(grouped01, "w1q01")
+        w1_q[0] = [quantize(grouped00, "w1q00", (0, P, 2 * P, PASS)), q01]
 
-        w2raw1 = load_w2(1)
-        raw10 = load_w1(1, 0, 0, PASS)
-        raw11 = [load_w1(1, 1, 0, 256, "tab0"), load_w1(1, 1, 256, PASS, "w1late")]
-
-        z_rows = [held.tile([P, PACK, PAIRS], BF16, name="z_rows%d" % g) for g in range(2)]
-        z_q = []
+        last = 2 * PACK - 1
         picked = None
         for i in range(2 * PACK):
-            if i + 1 < 2 * PACK:
+            if i == 2:
+                grouped1 = big.tile([P, 2 * PASS * PACK], BF16, name="grouped1", tag="root_then_w1", align_bytes=64)
+                round_w1(nc.scalar.copy, grouped1[:, : PASS * PACK], raw10, 0, PASS)
+                round_w1(nc.scalar.copy, grouped1[:, PASS * PACK :], raw11, 0, PASS)
+                load_sb = big.tile([P, N // P, PAIRS], F32, name="load_sb", tag="tab1", align_bytes=64)
+                nc.sync.dma_start(out=load_sb[:], in_=load.rearrange("(c p) m -> p c m", p=P))
+            if i < last:
                 damps[i + 1] = damping(i + 1, [(0, 1)])
+            if i == last - 1:
+                z_grouped0 = weave_z(nc.scalar.copy, 0, 0, PAIRS, "root_then_z")
             h = features(i, damps[i])
             if i > 0:
-                lower(i - 1, z_rows[(i - 1) // PACK], picked)
-            picked = pick(h)
+                lower(i - 1, picked[0], picked[1], 0, PAIRS)
+            if i < last:
+                picked = (pick(h, pos1_sb, "inlet", 0, PAIRS), pick(h, pos2_sb, "outlet", 0, PAIRS))
             if i == 0:
-                planes1 = deal_w2_planes(1)
                 words1 = deal_w2_words(1, w2raw1)
-                w2_q[1] = [(words1[:, a, :], planes1[:, a, :]) for a in range(2)]
-                grouped10 = ring.tile([P, PASS * PACK], BF16, name="grouped", align_bytes=64)
-                round_w1(nc.scalar.copy, grouped10, raw10, 0, PASS)
-            if i == 1:
-                q10 = quantize(grouped10, "w1q10")
-                grouped11 = ring.tile([P, PASS * PACK], BF16, name="grouped", align_bytes=64)
-                round_w1(nc.scalar.copy, grouped11, raw11[0], 0, 256)
-                round_w1(nc.scalar.copy, grouped11, raw11[1], 256, PASS)
-            if i == 2:
-                w1_q[1] = [q10, quantize(grouped11, "w1q11")]
-                load_sb = big.tile([P, N // P, PAIRS], F32, name="load_sb", tag="w1raw", align_bytes=64)
-                nc.sync.dma_start(out=load_sb[:], in_=load.rearrange("(c p) m -> p c m", p=P))
-                w4_sb = big.tile([P, 2, N], U16, name="w4_sb", tag="tab0", align_bytes=64)
+                w2_q[1] = [(words1[:, a, :], planes[a][:, S + PASS : S + H]) for a in range(2)]
+                w4_sb = big.tile([P, 2, N], U16, name="w4_sb", tag="w2raw", align_bytes=64)
                 nc.sync.dma_start(out=w4_sb[:].bitcast(I32), in_=w4_words.rearrange("a p c -> p a c").bitcast(I32))
-                w4_planes = big.tile([P, 2, N], U8, name="w4_planes", tag="tab_bytes", align_bytes=64)
-                load_planes(nc.sync, w4_planes, w4_scales)
-                bias_sb = big.tile([P, N // P], F32, name="bias_sb", tag="w1late", align_bytes=64)
+                w4_planes = big.tile([P, 2, N], U8, name="w4_planes", tag="tab0", align_bytes=64)
+                nc.vector.memset(w4_planes[:].rearrange("p a c -> p (a c)").bitcast(I32), 0)
+                for q in range(4):
+                    nc.sync.dma_start(
+                        out=w4_planes[32 * q : 32 * q + 4, :, :].bitcast(I32),
+                        in_=w4_scales[:, 4 * q : 4 * q + 4, :].rearrange("a r c -> r a c").bitcast(I32),
+                    )
+                bias_sb = big.tile([P, N // P], F32, name="bias_sb", tag="w1raw", align_bytes=64)
                 with nc.allow_non_contiguous_dma("one bias value to a partition"):
                     nc.sync.dma_start(out=bias_sb[:], in_=bias.rearrange("(c p) -> p c", p=P))
-            if i == PACK:
-                z_grouped0 = ring.tile([P, PAIRS * PACK], BF16, name="grouped", align_bytes=64)
-                weave_z(nc.scalar.copy, z_grouped0, z_rows[0], 0, PAIRS)
-            if i == PACK + 1:
-                z_q.append(quantize(z_grouped0, "zq0"))
-        lower(2 * PACK - 1, z_rows[1], picked)
-        z_grouped1 = ring.tile([P, PAIRS * PACK], BF16, name="grouped", align_bytes=64)
-        weave_z(nc.scalar.copy, z_grouped1, z_rows[1], 0, 192)
-        weave_z(nc.vector.tensor_copy, z_grouped1, z_rows[1], 192, PAIRS)
-        z_q.append(quantize(z_grouped1, "zq1"))
+            if i == 2:
+                codes1, plane1 = quantize(grouped1, "w1q1", (0, 2 * PASS))
+                w1_q[1] = [(codes1[:, a * PASS : (a + 1) * PASS], plane1[:, a * PASS : (a + 1) * PASS]) for a in range(2)]
 
-        ys = [psum.tile([P, BANK], F32, name="y", tag="b") for c in range(N // P)]
-        for g in range(2):
-            for c in range(N // P):
-                codes, plane = z_q[g]
+        pieces = [(m0, m0 + P) for m0 in range(0, PAIRS, P)]
+        inlets, outlets, woven = {}, {}, {}
+        outlets[0] = pick(h, pos2_sb, "outlet", *pieces[0])
+        for u, (m0, m1) in enumerate(pieces):
+            inlets[u] = pick(h, pos1_sb, "inlet", m0, m1)
+            if u + 1 < len(pieces):
+                outlets[u + 1] = pick(h, pos2_sb, "outlet", *pieces[u + 1])
+            else:
+                z0_codes, z0_plane = quantize(z_grouped0, "zq0")
+            lower(last, inlets[u], outlets[u], m0, m1)
+            woven[u] = weave_z(nc.scalar.copy, 1, m0, m1, "z_piece%d" % u)
+
+        out_rows = out.rearrange("(c p) m -> p c m", p=P)
+        banks = []
+        for u, (m0, m1) in enumerate(pieces):
+            width = m1 - m0
+            for c0 in range(0, N // P, BANK // width):
+                y = psum.tile([P, BANK // width, width], F32, name="y", tag="a")
+                banks.append((u, c0, BANK // width, y))
+
+        def third_product(g, bank, codes, plane, first_col):
+            u, c0, chunks, y = bank
+            m0, m1 = pieces[u]
+            steps = [(c, m) for c in range(chunks) for m in range(m0, m1, P)]
+            for n, (c, m) in enumerate(steps):
+                rows = slice((c0 + c) * P, (c0 + c + 1) * P)
+                cols = slice(m - first_col, m - first_col + P)
                 nc.tensor.matmul_mx(
-                    out=ys[c][:],
-                    lhsT=w4_sb[:, g, c * P : (c + 1) * P].bitcast(FP4X4),
-                    lhsT_scale=w4_planes[:, g, c * P : (c + 1) * P],
-                    rhs=codes[:].bitcast(FP8X4),
-                    rhs_scale=plane[:],
-                    start=(g == 0),
-                    stop=(g == 1),
+                    out=y[:, c, m - m0 : m - m0 + P],
+                    lhsT=w4_sb[:, g, rows].bitcast(FP4X4),
+                    lhsT_scale=w4_planes[:, g, rows],
+                    rhs=codes[:, cols].bitcast(FP8X4),
+                    rhs_scale=plane[:, cols],
+                    start=(g == 0 and n == 0),
+                    stop=(g == 1 and n == len(steps) - 1),
                 )
-        for c in range(N // P):
-            weighted = ring.tile([P, PAIRS], F32, name="weighted", bufs=4)
-            score = ring.tile([P, PAIRS], F32, name="score", bufs=4)
-            nc.vector.tensor_tensor(weighted[:], ys[c][:], load_sb[:, c, :], ALU.mult)
-            nc.scalar.activation(score[:], weighted[:], ACT.Identity, bias=bias_sb[:, c : c + 1])
-            nc.sync.dma_start(out=out[c * P : (c + 1) * P, :], in_=score[:])
+
+        for bank in banks:
+            third_product(0, bank, z0_codes, z0_plane, 0)
+        z1_q = [quantize(woven[u], "zq1%d" % u, (0, m1 - m0)) for u, (m0, m1) in enumerate(pieces)]
+        for bank in banks:
+            u, c0, chunks, y = bank
+            m0, m1 = pieces[u]
+            third_product(1, bank, z1_q[u][0], z1_q[u][1], m0)
+            weighted = ring.tile([P, chunks, m1 - m0], F32, name="weighted", bufs=4)
+            score = ring.tile([P, chunks, m1 - m0], F32, name="score", bufs=4)
+            nc.vector.tensor_tensor(weighted[:], y[:], load_sb[:, c0 : c0 + chunks, m0:m1], ALU.mult)
+            for c in range(chunks):
+                nc.scalar.activation(
+                    score[:, c, :], weighted[:, c, :], ACT.Identity, bias=bias_sb[:, c0 + c : c0 + c + 1]
+                )
+            nc.sync.dma_start(out=out_rows[:, c0 : c0 + chunks, m0:m1], in_=score[:])

@@ -76,13 +76,15 @@ def tile_list_electrolyser_pair_minimum_kernel(
                 )
             return codes, plane
 
-        def deal_w2_words(g, raw):
-            dealt = held.tile([P, 2, PASS], I32, name="w2_dealt%d" % g, align_bytes=64)
+        def deal_w2_words(g, raw, t0, t1, tag):
+            dealt = big.tile([P, 2, (t1 - t0) * P], I32, name="w2_dealt", tag=tag, align_bytes=64)
             nc.vector.tensor_copy(
-                out=dealt[:].rearrange("p a (t c i) -> p a c t i", t=PACK, i=4),
-                in_=raw[:].rearrange("p a (c i t) -> p a c t i", t=PACK, i=4),
+                out=dealt[:].rearrange("p a (t c i) -> p a c t i", t=t1 - t0, i=4),
+                in_=raw[:].rearrange("p a (c i t) -> p a c t i", t=PACK, i=4)[:, :, :, t0:t1, :],
             )
-            return dealt
+            for t in range(t0, t1):
+                cols = slice(S + g * PASS + t * P, S + g * PASS + (t + 1) * P)
+                w2_q[g * PACK + t] = [(dealt[:, a, (t - t0) * P : (t - t0 + 1) * P], planes[a][:, cols]) for a in range(2)]
 
         v_words, v_planes = {}, {}
 
@@ -92,15 +94,15 @@ def tile_list_electrolyser_pair_minimum_kernel(
             nc.vector.tensor_copy(out=picked[:], in_=words[:].indirect(cols))
             v_words[a, half], v_planes[a, half] = picked, planes[a][:, half * BANK : (half + 1) * BANK]
 
-        def first_product(tag, operands, t, passes):
+        def first_product(tag, operands, passes):
             accs = [psum.tile([P, BANK], F32, name="acc", tag=tag) for half in range(2)]
             for a in passes:
                 codes, plane = operands[a]
                 for half in range(2):
                     nc.tensor.matmul_mx(
                         out=accs[half][:],
-                        lhsT=codes[:, t * P : (t + 1) * P].bitcast(FP8X4),
-                        lhsT_scale=plane[:, t * P : (t + 1) * P],
+                        lhsT=codes.bitcast(FP8X4),
+                        lhsT_scale=plane,
                         rhs=v_words[a, half][:].bitcast(FP4X4),
                         rhs_scale=v_planes[a, half],
                         start=(a == passes[0]),
@@ -113,14 +115,13 @@ def tile_list_electrolyser_pair_minimum_kernel(
         root_tags = {2: "root_then_w1", 2 * PACK - 1: "root_then_z"}
 
         def damping(i, spans):
-            g, t = divmod(i, PACK)
             size = ring.tile([P, S], F32, name="size")
             if i in root_tags:
                 root = big.tile([P, S], F32, name="root", tag=root_tags[i], align_bytes=64)
             else:
                 root = ring.tile([P, S], F32, name="root")
             damp = damp_all[:, i * S : (i + 1) * S]
-            b = first_product("b", w2_q[g], t, (0, 1))
+            b = first_product("b", w2_q[i], (0, 1))
             for span in spans:
                 for half in span:
                     nc.scalar.activation(size[:, half * BANK : (half + 1) * BANK], b[half][:], ACT.Abs)
@@ -132,7 +133,8 @@ def tile_list_electrolyser_pair_minimum_kernel(
         def features(i, damp):
             g, t = divmod(i, PACK)
             h = ring.tile([P, S], F32, name="h")
-            a_sum = first_product("a", w1_q[g], t, (1 - g, g))
+            operands = [(codes[:, t * P : (t + 1) * P], plane[:, t * P : (t + 1) * P]) for codes, plane in w1_q[g]]
+            a_sum = first_product("a", operands, (1 - g, g))
             for half in range(2):
                 cols = slice(half * BANK, (half + 1) * BANK)
                 nc.vector.tensor_tensor(h[:, cols], a_sum[half][:], damp[:, cols], ALU.mult)
@@ -164,17 +166,11 @@ def tile_list_electrolyser_pair_minimum_kernel(
         load_scale_rows(w2_bytes[0:32, :], w2_scales)
         for rows in (slice(32, 64), slice(64, 128)):
             nc.vector.memset(tab_bytes[rows, :].bitcast(I32), 0)
-            nc.vector.memset(w2_bytes[rows, :].bitcast(I32), 0)
-        nc.vector.memset(planes[1][:].bitcast(I32), 0)
+            nc.gpsimd.memset(w2_bytes[rows, :].bitcast(I32), 0)
+        nc.gpsimd.memset(planes[1][:].bitcast(I32), 0)
         tab0 = load_table(0)
         nc.sync.dma_start(pos1_sb[:], pos1)
         nc.sync.dma_start(pos2_sb[:], pos2)
-        gain_sb = held.tile([P, 2 * PACK], F32, name="gain_sb")
-        with nc.allow_non_contiguous_dma("four gains to a partition and group"):
-            nc.sync.dma_start(
-                out=gain_sb[:].rearrange("p (g t) -> p g t", t=PACK),
-                in_=gain.rearrange("(g p t) -> p g t", p=P, t=PACK),
-            )
         w2raw = load_w2(0)
         raw00a = load_w1(0, 0, 0, half_cols, "w1raw")
         tab1 = load_table(1)
@@ -198,21 +194,27 @@ def tile_list_electrolyser_pair_minimum_kernel(
         gather_table(tab0, 0, 0)
         gather_table(tab0, 0, 1)
         raw00b = load_w1(0, 0, half_cols, PASS, "tab0")
-        grouped00 = ring.tile([P, PASS * PACK], BF16, name="grouped", align_bytes=64)
+        grouped00 = big.tile([P, PASS * PACK], BF16, name="grouped00", tag="w1_then_w2", align_bytes=64)
         round_w1(nc.scalar.copy, grouped00[:], raw00a, 0, half_cols)
-        words0 = deal_w2_words(0, w2raw)
-        w2_q[0] = [(words0[:, a, :], planes[a][:, S : S + PASS]) for a in range(2)]
-        w2raw1 = load_w2(1)
+        deal_w2_words(0, w2raw, 0, 2, "w2_dealt_first")
         gather_table(tab1, 1, 0)
         gather_table(tab1, 1, 1)
         raw10 = load_w1(1, 0, 0, PASS, "tab1")
         damps = {0: damping(0, [(0,), (1,)])}
-        grouped01 = ring.tile([P, PASS * PACK], BF16, name="grouped", align_bytes=64)
+        grouped01 = big.tile([P, PASS * PACK], BF16, name="grouped01", tag="w1_then_gain", align_bytes=64)
         round_w1(nc.vector.tensor_copy, grouped01[:], raw01, 0, PASS)
         raw11 = load_w1(1, 1, 0, PASS, "v_bytes")
         round_w1(nc.vector.tensor_copy, grouped00[:], raw00b, half_cols, PASS)
         q01 = quantize(grouped01, "w1q01")
         w1_q[0] = [quantize(grouped00, "w1q00", (0, P, 2 * P, PASS)), q01]
+        deal_w2_words(0, w2raw, 2, PACK, "w1_then_w2")
+        gain_sb = big.tile([P, 2 * PACK], F32, name="gain_sb", tag="w1_then_gain", align_bytes=64)
+        with nc.allow_non_contiguous_dma("four gains to a partition and group"):
+            nc.sync.dma_start(
+                out=gain_sb[:].rearrange("p (g t) -> p g t", t=PACK),
+                in_=gain.rearrange("(g p t) -> p g t", p=P, t=PACK),
+            )
+        w2raw1 = load_w2(1)
 
         last = 2 * PACK - 1
         picked = None
@@ -223,6 +225,9 @@ def tile_list_electrolyser_pair_minimum_kernel(
                 round_w1(nc.scalar.copy, grouped1[:, PASS * PACK :], raw11, 0, PASS)
                 load_sb = big.tile([P, N // P, PAIRS], F32, name="load_sb", tag="tab1", align_bytes=64)
                 nc.sync.dma_start(out=load_sb[:], in_=load.rearrange("(c p) m -> p c m", p=P))
+                bias_sb = big.tile([P, N // P], F32, name="bias_sb", tag="v_bytes", align_bytes=64)
+                with nc.allow_non_contiguous_dma("one bias value to a partition"):
+                    nc.sync.dma_start(out=bias_sb[:], in_=bias.rearrange("(c p) -> p c", p=P))
             if i < last:
                 damps[i + 1] = damping(i + 1, [(0, 1)])
             if i == last - 1:
@@ -233,8 +238,7 @@ def tile_list_electrolyser_pair_minimum_kernel(
             if i < last:
                 picked = (pick(h, pos1_sb, "inlet", 0, PAIRS), pick(h, pos2_sb, "outlet", 0, PAIRS))
             if i == 0:
-                words1 = deal_w2_words(1, w2raw1)
-                w2_q[1] = [(words1[:, a, :], planes[a][:, S + PASS : S + H]) for a in range(2)]
+                deal_w2_words(1, w2raw1, 0, PACK, "w2_dealt_second")
                 w4_sb = big.tile([P, 2, N], U16, name="w4_sb", tag="w2raw", align_bytes=64)
                 nc.sync.dma_start(out=w4_sb[:].bitcast(I32), in_=w4_words.rearrange("a p c -> p a c").bitcast(I32))
                 w4_planes = big.tile([P, 2, N], U8, name="w4_planes", tag="tab0", align_bytes=64)
@@ -244,22 +248,18 @@ def tile_list_electrolyser_pair_minimum_kernel(
                         out=w4_planes[32 * q : 32 * q + 4, :, :].bitcast(I32),
                         in_=w4_scales[:, 4 * q : 4 * q + 4, :].rearrange("a r c -> r a c").bitcast(I32),
                     )
-                bias_sb = big.tile([P, N // P], F32, name="bias_sb", tag="w1raw", align_bytes=64)
-                with nc.allow_non_contiguous_dma("one bias value to a partition"):
-                    nc.sync.dma_start(out=bias_sb[:], in_=bias.rearrange("(c p) -> p c", p=P))
             if i == 2:
                 codes1, plane1 = quantize(grouped1, "w1q1", (0, 2 * PASS))
                 w1_q[1] = [(codes1[:, a * PASS : (a + 1) * PASS], plane1[:, a * PASS : (a + 1) * PASS]) for a in range(2)]
 
         pieces = [(m0, m0 + P) for m0 in range(0, PAIRS, P)]
+        z0_codes, z0_plane = quantize(z_grouped0, "zq0")
         inlets, outlets, woven = {}, {}, {}
         outlets[0] = pick(h, pos2_sb, "outlet", *pieces[0])
         for u, (m0, m1) in enumerate(pieces):
             inlets[u] = pick(h, pos1_sb, "inlet", m0, m1)
             if u + 1 < len(pieces):
                 outlets[u + 1] = pick(h, pos2_sb, "outlet", *pieces[u + 1])
-            else:
-                z0_codes, z0_plane = quantize(z_grouped0, "zq0")
             lower(last, inlets[u], outlets[u], m0, m1)
             woven[u] = weave_z(nc.scalar.copy, 1, m0, m1, "z_piece%d" % u)
 
@@ -268,7 +268,7 @@ def tile_list_electrolyser_pair_minimum_kernel(
         for u, (m0, m1) in enumerate(pieces):
             width = m1 - m0
             for c0 in range(0, N // P, BANK // width):
-                y = psum.tile([P, BANK // width, width], F32, name="y", tag="a")
+                y = psum.tile([P, BANK // width, width], F32, name="y", tag="b")
                 banks.append((u, c0, BANK // width, y))
 
         def third_product(g, bank, codes, plane, first_col):

@@ -20,6 +20,11 @@ P = 128
 PACK = 4
 PASS = P * PACK
 BANK = 512
+ROW_TILES = H // P
+LAST = ROW_TILES - 1
+HALF = PASS // 2
+RUN = 4
+ROUND_AFTER = 2
 
 
 def tile_list_electrolyser_pair_minimum_kernel(
@@ -38,37 +43,39 @@ def tile_list_electrolyser_pair_minimum_kernel(
 
         tab_bytes = big.tile([P, T], U8, name="tab_bytes", tag="tab_bytes", align_bytes=64)
         w2_bytes = big.tile([P, H], U8, name="w2_bytes", tag="w2_bytes", align_bytes=64)
-        planes = [held.tile([P, S + H], U8, name="planes%d" % a, align_bytes=64) for a in range(2)]
+        planes = [held.tile([P, S + H], U8, name="planes%d" % kp, align_bytes=64) for kp in range(2)]
+
         warm = held.tile([P, 2], F32, name="warm")
         nc.vector.memset(warm[:, 0:1], 1.0)
         nc.scalar.activation(warm[:, 1:2], warm[:, 0:1], ACT.Abs_reciprocal_sqrt)
+        one = warm[:, 1:2]
 
         def load_scale_rows(dst, scales):
-            nc.sync.dma_start(out=dst.bitcast(I32), in_=scales.rearrange("a q c -> (a q) c").bitcast(I32))
+            nc.sync.dma_start(out=dst.bitcast(I32), in_=scales.rearrange("kp u c -> (kp u) c").bitcast(I32))
 
-        def load_table(a):
-            words = big.tile([P, T], U16, name="tab_w", tag="tab%d" % a, align_bytes=64)
-            nc.sync.dma_start(out=words[:].bitcast(I32), in_=tab_words[a].bitcast(I32))
+        def load_table(kp):
+            words = big.tile([P, T], U16, name="tab_w", tag="tab%d" % kp, align_bytes=64)
+            nc.sync.dma_start(out=words[:].bitcast(I32), in_=tab_words[kp].bitcast(I32))
             return words
 
-        def load_w1(g, a, c0, c1, tag):
+        def load_w1(g, kp, c0, c1, tag):
             raw = big.tile([P, PACK, c1 - c0], F32, name="w1_raw", tag=tag, align_bytes=64)
-            rows = w1[a * PASS : (a + 1) * PASS, g * PASS + c0 : g * PASS + c1]
+            rows = w1[kp * PASS : (kp + 1) * PASS, g * PASS + c0 : g * PASS + c1]
             nc.sync.dma_start(out=raw[:], in_=rows.rearrange("(p j) c -> p j c", j=PACK))
             return raw
 
         def load_w2(g):
             raw = big.tile([P, 2, PASS], I32, name="w2_raw", tag="w2raw", align_bytes=64)
-            src = w2_words[:, :, g * PASS : (g + 1) * PASS, :].rearrange("a p c i -> p a (c i)")
+            src = w2_words[:, :, g * PASS : (g + 1) * PASS, :].rearrange("kp p c j -> p kp (c j)")
             nc.sync.dma_start(out=raw[:], in_=src.bitcast(I32))
             return raw
 
         def round_w1(copy, grouped, raw, c0, c1):
             dst = grouped.rearrange("p (t m j) -> p m j t", t=PACK, j=PACK)[:, c0 // PACK : c1 // PACK]
-            copy(out=dst, in_=raw[:].rearrange("p j (m t) -> p m j t", t=PACK))
+            copy(out=dst, in_=raw.rearrange("p j (m t) -> p m j t", t=PACK))
 
-        def quantize(grouped, name, cuts=(0, PASS)):
-            codes = held.tile([P, cuts[-1]], U32, name=name + "_codes", align_bytes=64)
+        def quantize(grouped, name, cuts):
+            codes = big.tile([P, cuts[-1]], U32, name="codes", tag=name, align_bytes=64)
             plane = held.tile([P, cuts[-1]], U8, name=name + "_plane", align_bytes=64)
             for c0, c1 in zip(cuts, cuts[1:]):
                 nc.vector.quantize_mx(
@@ -76,43 +83,42 @@ def tile_list_electrolyser_pair_minimum_kernel(
                 )
             return codes, plane
 
+        v_words, w1_q, w2_q = {}, {}, {}
+
         def deal_w2_words(g, raw, t0, t1, tag):
             dealt = big.tile([P, 2, (t1 - t0) * P], I32, name="w2_dealt", tag=tag, align_bytes=64)
             nc.vector.tensor_copy(
-                out=dealt[:].rearrange("p a (t c i) -> p a c t i", t=t1 - t0, i=4),
-                in_=raw[:].rearrange("p a (c i t) -> p a c t i", t=PACK, i=4)[:, :, :, t0:t1, :],
+                out=dealt[:].rearrange("p kp (t c e) -> p kp c t e", t=t1 - t0, e=RUN),
+                in_=raw[:].rearrange("p kp (c e t) -> p kp c t e", t=PACK, e=RUN)[:, :, :, t0:t1, :],
             )
             for t in range(t0, t1):
                 cols = slice(S + g * PASS + t * P, S + g * PASS + (t + 1) * P)
-                w2_q[g * PACK + t] = [(dealt[:, a, (t - t0) * P : (t - t0 + 1) * P], planes[a][:, cols]) for a in range(2)]
+                words = dealt[:, :, (t - t0) * P : (t - t0 + 1) * P]
+                w2_q[g * PACK + t] = [(words[:, kp, :], planes[kp][:, cols]) for kp in range(2)]
 
-        v_words, v_planes = {}, {}
-
-        def gather_table(words, a, half):
+        def gather_table(words, kp, half):
             cols = offs_sb[:, half * BANK // 16 : (half + 1) * BANK // 16]
-            picked = held.tile([P, BANK], U16, name="v_words%d%d" % (a, half), align_bytes=64)
-            nc.vector.tensor_copy(out=picked[:], in_=words[:].indirect(cols))
-            v_words[a, half], v_planes[a, half] = picked, planes[a][:, half * BANK : (half + 1) * BANK]
+            v_words[kp, half] = held.tile([P, BANK], U16, name="v_words%d%d" % (kp, half), align_bytes=64)
+            nc.vector.tensor_copy(out=v_words[kp, half][:], in_=words[:].indirect(cols))
 
         def first_product(tag, operands, passes):
-            accs = [psum.tile([P, BANK], F32, name="acc", tag=tag) for half in range(2)]
-            for a in passes:
-                codes, plane = operands[a]
+            sums = [psum.tile([P, BANK], F32, name="acc", tag=tag) for half in range(2)]
+            for kp in passes:
+                codes, plane = operands[kp]
                 for half in range(2):
                     nc.tensor.matmul_mx(
-                        out=accs[half][:],
+                        out=sums[half][:],
                         lhsT=codes.bitcast(FP8X4),
                         lhsT_scale=plane,
-                        rhs=v_words[a, half][:].bitcast(FP4X4),
-                        rhs_scale=v_planes[a, half],
-                        start=(a == passes[0]),
-                        stop=(a == passes[1]),
+                        rhs=v_words[kp, half][:].bitcast(FP4X4),
+                        rhs_scale=planes[kp][:, half * BANK : (half + 1) * BANK],
+                        start=(kp == passes[0]),
+                        stop=(kp == passes[1]),
                     )
-            return accs
+            return sums
 
-        w1_q, w2_q = {}, {}
-        damp_all = held.tile([P, (2 * PACK + 1) * S], F32, name="damp_all")
-        root_tags = {2: "root_then_w1", 2 * PACK - 1: "root_then_z"}
+        damp_all = held.tile([P, (ROW_TILES + 1) * S], F32, name="damp_all")
+        root_tags = {ROUND_AFTER: "root_then_w1", LAST: "root_then_z"}
 
         def damping(i, spans):
             size = ring.tile([P, S], F32, name="size")
@@ -121,23 +127,22 @@ def tile_list_electrolyser_pair_minimum_kernel(
             else:
                 root = ring.tile([P, S], F32, name="root")
             damp = damp_all[:, i * S : (i + 1) * S]
-            b = first_product("b", w2_q[i], (0, 1))
+            b_sums = first_product("b", w2_q[i], (0, 1))
             for span in spans:
                 for half in span:
-                    nc.scalar.activation(size[:, half * BANK : (half + 1) * BANK], b[half][:], ACT.Abs)
+                    nc.scalar.activation(size[:, half * BANK : (half + 1) * BANK], b_sums[half][:], ACT.Abs)
                 cols = slice(span[0] * BANK, (span[-1] + 1) * BANK)
-                nc.scalar.activation(root[:, cols], size[:, cols], ACT.Abs_reciprocal_sqrt, bias=1.0)
+                nc.scalar.activation(root[:, cols], size[:, cols], ACT.Abs_reciprocal_sqrt, bias=one)
                 nc.scalar.activation(damp[:, cols], root[:, cols], ACT.Square)
-            return damp
 
-        def features(i, damp):
+        def features(i):
             g, t = divmod(i, PACK)
             h = ring.tile([P, S], F32, name="h")
             operands = [(codes[:, t * P : (t + 1) * P], plane[:, t * P : (t + 1) * P]) for codes, plane in w1_q[g]]
-            a_sum = first_product("a", operands, (1 - g, g))
+            a_sums = first_product("a", operands, (1 - g, g))
             for half in range(2):
-                cols = slice(half * BANK, (half + 1) * BANK)
-                nc.vector.tensor_tensor(h[:, cols], a_sum[half][:], damp[:, cols], ALU.mult)
+                c0, c1 = half * BANK, (half + 1) * BANK
+                nc.vector.tensor_tensor(h[:, c0:c1], a_sums[half][:], damp_all[:, i * S + c0 : i * S + c1], ALU.mult)
             return h
 
         def pick(h, pos_sb, name, m0, m1):
@@ -147,20 +152,23 @@ def tile_list_electrolyser_pair_minimum_kernel(
 
         def lower(i, inlet, outlet, m0, m1):
             nc.vector.scalar_tensor_tensor(
-                out=damp_all[:, (i + 1) * S + m0 : (i + 1) * S + m1], in0=outlet[:], scalar=gain_sb[:, i : i + 1], in1=inlet[:],
-                op0=ALU.mult, op1=ALU.min,
+                out=damp_all[:, (i + 1) * S + m0 : (i + 1) * S + m1],
+                in0=outlet[:],
+                scalar=gain_sb[:, i : i + 1],
+                in1=inlet[:],
+                op0=ALU.mult,
+                op1=ALU.min,
             )
 
-        def weave_z(copy, g, m0, m1, tag):
+        def interleave_z(g, m0, m1, tag):
             grouped = big.tile([P, (m1 - m0) * PACK], BF16, name="grouped", tag=tag, align_bytes=64)
             z_rows = damp_all[:, (g * PACK + 1) * S : (g * PACK + PACK + 1) * S].rearrange("p (t s) -> p t s", t=PACK)
-            copy(
-                out=grouped[:].rearrange("p (c i t) -> p c t i", t=PACK, i=4),
-                in_=z_rows[:, :, m0:m1].rearrange("p t (c i) -> p c t i", i=4),
+            nc.scalar.copy(
+                out=grouped[:].rearrange("p (c e t) -> p c t e", t=PACK, e=RUN),
+                in_=z_rows[:, :, m0:m1].rearrange("p t (c e) -> p c t e", e=RUN),
             )
             return grouped
 
-        half_cols = PASS // 2
         nc.sync.dma_start(offs_sb[:], offs)
         load_scale_rows(tab_bytes[0:32, :], tab_scales)
         load_scale_rows(w2_bytes[0:32, :], w2_scales)
@@ -171,8 +179,8 @@ def tile_list_electrolyser_pair_minimum_kernel(
         tab0 = load_table(0)
         nc.sync.dma_start(pos1_sb[:], pos1)
         nc.sync.dma_start(pos2_sb[:], pos2)
-        w2raw = load_w2(0)
-        raw00a = load_w1(0, 0, 0, half_cols, "w1raw")
+        w2raw0 = load_w2(0)
+        raw00_left = load_w1(0, 0, 0, HALF, "w1raw")
         tab1 = load_table(1)
 
         v_bytes = big.tile([P, S], U8, name="v_bytes", tag="v_bytes", align_bytes=64)
@@ -182,33 +190,33 @@ def tile_list_electrolyser_pair_minimum_kernel(
             in_=w2_bytes[:].rearrange("p (g m t) -> p g m t", g=2, t=PACK),
         )
         nc.vector.tensor_copy(out=planes[0][:, 0:S].bitcast(I32), in_=v_bytes[:].bitcast(I32))
-        for a in range(2):
-            for q in range(1 - a, 4):
-                row = 16 * a + 4 * q
-                queue = nc.gpsimd if (a, q) == (1, 3) else nc.sync
-                queue.dma_start(
-                    out=planes[a][32 * q : 32 * q + 4, :].bitcast(I32), in_=planes[0][row : row + 4, :].bitcast(I32)
-                )
+        moves = [(kp, q) for kp in range(2) for q in range(1 - kp, 4)]
+        for kp, q in moves:
+            row = 16 * kp + 4 * q
+            queue = nc.gpsimd if (kp, q) == moves[-1] else nc.sync
+            queue.dma_start(
+                out=planes[kp][32 * q : 32 * q + 4, :].bitcast(I32), in_=planes[0][row : row + 4, :].bitcast(I32)
+            )
         raw01 = load_w1(0, 1, 0, PASS, "v_bytes")
 
         gather_table(tab0, 0, 0)
         gather_table(tab0, 0, 1)
-        raw00b = load_w1(0, 0, half_cols, PASS, "tab0")
+        raw00_right = load_w1(0, 0, HALF, PASS, "tab0")
         grouped00 = big.tile([P, PASS * PACK], BF16, name="grouped00", tag="w1_then_w2", align_bytes=64)
-        round_w1(nc.scalar.copy, grouped00[:], raw00a, 0, half_cols)
-        deal_w2_words(0, w2raw, 0, 2, "w2_dealt_first")
+        round_w1(nc.scalar.copy, grouped00[:], raw00_left[:], 0, HALF)
+        deal_w2_words(0, w2raw0, 0, 2, "w2_dealt_first")
         gather_table(tab1, 1, 0)
         gather_table(tab1, 1, 1)
         raw10 = load_w1(1, 0, 0, PASS, "tab1")
-        damps = {0: damping(0, [(0,), (1,)])}
+        damping(0, [(0,), (1,)])
         grouped01 = big.tile([P, PASS * PACK], BF16, name="grouped01", tag="w1_then_gain", align_bytes=64)
-        round_w1(nc.vector.tensor_copy, grouped01[:], raw01, 0, PASS)
+        round_w1(nc.vector.tensor_copy, grouped01[:], raw01[:], 0, PASS)
         raw11 = load_w1(1, 1, 0, PASS, "v_bytes")
-        round_w1(nc.vector.tensor_copy, grouped00[:], raw00b, half_cols, PASS)
-        q01 = quantize(grouped01, "w1q01")
+        round_w1(nc.vector.tensor_copy, grouped00[:], raw00_right[:], HALF, PASS)
+        q01 = quantize(grouped01, "w1q01", (0, PASS))
         w1_q[0] = [quantize(grouped00, "w1q00", (0, P, 2 * P, PASS)), q01]
-        deal_w2_words(0, w2raw, 2, PACK, "w1_then_w2")
-        gain_sb = big.tile([P, 2 * PACK], F32, name="gain_sb", tag="w1_then_gain", align_bytes=64)
+        deal_w2_words(0, w2raw0, 2, PACK, "w1_then_w2")
+        gain_sb = big.tile([P, ROW_TILES], F32, name="gain_sb", tag="w1_then_gain", align_bytes=64)
         with nc.allow_non_contiguous_dma("four gains to a partition and group"):
             nc.sync.dma_start(
                 out=gain_sb[:].rearrange("p (g t) -> p g t", t=PACK),
@@ -216,90 +224,79 @@ def tile_list_electrolyser_pair_minimum_kernel(
             )
         w2raw1 = load_w2(1)
 
-        last = 2 * PACK - 1
         picked = None
-        for i in range(2 * PACK):
-            if i == 2:
+        for i in range(ROW_TILES):
+            if i == ROUND_AFTER:
                 grouped1 = big.tile([P, 2 * PASS * PACK], BF16, name="grouped1", tag="root_then_w1", align_bytes=64)
-                round_w1(nc.scalar.copy, grouped1[:, : PASS * PACK], raw10, 0, PASS)
-                round_w1(nc.scalar.copy, grouped1[:, PASS * PACK :], raw11, 0, PASS)
+                round_w1(nc.scalar.copy, grouped1[:, : PASS * PACK], raw10[:], 0, PASS)
+                round_w1(nc.scalar.copy, grouped1[:, PASS * PACK :], raw11[:, :, :HALF], 0, HALF)
                 load_sb = big.tile([P, N // P, PAIRS], F32, name="load_sb", tag="tab1", align_bytes=64)
                 nc.sync.dma_start(out=load_sb[:], in_=load.rearrange("(c p) m -> p c m", p=P))
-                bias_sb = big.tile([P, N // P], F32, name="bias_sb", tag="v_bytes", align_bytes=64)
-                with nc.allow_non_contiguous_dma("one bias value to a partition"):
-                    nc.sync.dma_start(out=bias_sb[:], in_=bias.rearrange("(c p) -> p c", p=P))
-            if i < last:
-                damps[i + 1] = damping(i + 1, [(0, 1)])
-            if i == last - 1:
-                z_grouped0 = weave_z(nc.scalar.copy, 0, 0, PAIRS, "root_then_z")
-            h = features(i, damps[i])
+            if i < LAST:
+                damping(i + 1, [(0, 1)])
+            if i == LAST - 1:
+                z_grouped0 = interleave_z(0, 0, PAIRS, "root_then_z")
+            h = features(i)
             if i > 0:
                 lower(i - 1, picked[0], picked[1], 0, PAIRS)
-            if i < last:
+            if i < LAST:
                 picked = (pick(h, pos1_sb, "inlet", 0, PAIRS), pick(h, pos2_sb, "outlet", 0, PAIRS))
             if i == 0:
                 deal_w2_words(1, w2raw1, 0, PACK, "w2_dealt_second")
                 w4_sb = big.tile([P, 2, N], U16, name="w4_sb", tag="w2raw", align_bytes=64)
-                nc.sync.dma_start(out=w4_sb[:].bitcast(I32), in_=w4_words.rearrange("a p c -> p a c").bitcast(I32))
+                nc.sync.dma_start(out=w4_sb[:].bitcast(I32), in_=w4_words.rearrange("kp p c -> p kp c").bitcast(I32))
                 w4_planes = big.tile([P, 2, N], U8, name="w4_planes", tag="tab0", align_bytes=64)
-                nc.vector.memset(w4_planes[:].rearrange("p a c -> p (a c)").bitcast(I32), 0)
+                nc.vector.memset(w4_planes[:].rearrange("p kp c -> p (kp c)").bitcast(I32), 0)
                 for q in range(4):
                     nc.sync.dma_start(
                         out=w4_planes[32 * q : 32 * q + 4, :, :].bitcast(I32),
-                        in_=w4_scales[:, 4 * q : 4 * q + 4, :].rearrange("a r c -> r a c").bitcast(I32),
+                        in_=w4_scales[:, 4 * q : 4 * q + 4, :].rearrange("kp r c -> r kp c").bitcast(I32),
                     )
-            if i == 2:
+            if i == ROUND_AFTER:
+                round_w1(nc.vector.tensor_copy, grouped1[:, PASS * PACK :], raw11[:, :, HALF:], HALF, PASS)
+                bias_sb = big.tile([P, N // P], F32, name="bias_sb", tag="v_bytes", align_bytes=64)
+                with nc.allow_non_contiguous_dma("one bias value to a partition"):
+                    nc.sync.dma_start(out=bias_sb[:], in_=bias.rearrange("(c p) -> p c", p=P))
                 codes1, plane1 = quantize(grouped1, "w1q1", (0, 2 * PASS))
-                w1_q[1] = [(codes1[:, a * PASS : (a + 1) * PASS], plane1[:, a * PASS : (a + 1) * PASS]) for a in range(2)]
+                w1_q[1] = [
+                    (codes1[:, kp * PASS : (kp + 1) * PASS], plane1[:, kp * PASS : (kp + 1) * PASS]) for kp in range(2)
+                ]
 
-        pieces = [(m0, m0 + P) for m0 in range(0, PAIRS, P)]
-        z0_codes, z0_plane = quantize(z_grouped0, "zq0")
-        inlets, outlets, woven = {}, {}, {}
-        outlets[0] = pick(h, pos2_sb, "outlet", *pieces[0])
-        for u, (m0, m1) in enumerate(pieces):
-            inlets[u] = pick(h, pos1_sb, "inlet", m0, m1)
-            if u + 1 < len(pieces):
-                outlets[u + 1] = pick(h, pos2_sb, "outlet", *pieces[u + 1])
-            lower(last, inlets[u], outlets[u], m0, m1)
-            woven[u] = weave_z(nc.scalar.copy, 1, m0, m1, "z_piece%d" % u)
+        starts = list(range(0, PAIRS, P))
+        z0_codes, z0_plane = quantize(z_grouped0, "zq0", (0, PAIRS))
+        outlet = pick(h, pos2_sb, "outlet", 0, P)
+        z1_grouped = []
+        for m0 in starts:
+            inlet = pick(h, pos1_sb, "inlet", m0, m0 + P)
+            next_outlet = pick(h, pos2_sb, "outlet", m0 + P, m0 + 2 * P) if m0 < starts[-1] else None
+            lower(LAST, inlet, outlet, m0, m0 + P)
+            z1_grouped.append(interleave_z(1, m0, m0 + P, "z_piece%d" % (m0 // P)))
+            outlet = next_outlet
 
-        out_rows = out.rearrange("(c p) m -> p c m", p=P)
-        banks = []
-        for u, (m0, m1) in enumerate(pieces):
-            width = m1 - m0
-            for c0 in range(0, N // P, BANK // width):
-                y = psum.tile([P, BANK // width, width], F32, name="y", tag="b")
-                banks.append((u, c0, BANK // width, y))
+        chunks = N // P
+        banks = [psum.tile([P, chunks, P], F32, name="y", tag="b") for m0 in starts]
 
-        def third_product(g, bank, codes, plane, first_col):
-            u, c0, chunks, y = bank
-            m0, m1 = pieces[u]
-            steps = [(c, m) for c in range(chunks) for m in range(m0, m1, P)]
-            for n, (c, m) in enumerate(steps):
-                rows = slice((c0 + c) * P, (c0 + c + 1) * P)
-                cols = slice(m - first_col, m - first_col + P)
-                nc.tensor.matmul_mx(
-                    out=y[:, c, m - m0 : m - m0 + P],
-                    lhsT=w4_sb[:, g, rows].bitcast(FP4X4),
-                    lhsT_scale=w4_planes[:, g, rows],
-                    rhs=codes[:, cols].bitcast(FP8X4),
-                    rhs_scale=plane[:, cols],
-                    start=(g == 0 and n == 0),
-                    stop=(g == 1 and n == len(steps) - 1),
-                )
-
-        for bank in banks:
-            third_product(0, bank, z0_codes, z0_plane, 0)
-        z1_q = [quantize(woven[u], "zq1%d" % u, (0, m1 - m0)) for u, (m0, m1) in enumerate(pieces)]
-        for bank in banks:
-            u, c0, chunks, y = bank
-            m0, m1 = pieces[u]
-            third_product(1, bank, z1_q[u][0], z1_q[u][1], m0)
-            weighted = ring.tile([P, chunks, m1 - m0], F32, name="weighted", bufs=4)
-            score = ring.tile([P, chunks, m1 - m0], F32, name="score", bufs=4)
-            nc.vector.tensor_tensor(weighted[:], y[:], load_sb[:, c0 : c0 + chunks, m0:m1], ALU.mult)
+        def third_product(g, y, codes, plane):
             for c in range(chunks):
-                nc.scalar.activation(
-                    score[:, c, :], weighted[:, c, :], ACT.Identity, bias=bias_sb[:, c0 + c : c0 + c + 1]
+                nc.tensor.matmul_mx(
+                    out=y[:, c, :],
+                    lhsT=w4_sb[:, g, c * P : (c + 1) * P].bitcast(FP4X4),
+                    lhsT_scale=w4_planes[:, g, c * P : (c + 1) * P],
+                    rhs=codes.bitcast(FP8X4),
+                    rhs_scale=plane,
+                    start=(g == 0 and c == 0),
+                    stop=(g == 1 and c == chunks - 1),
                 )
-            nc.sync.dma_start(out=out_rows[:, c0 : c0 + chunks, m0:m1], in_=score[:])
+
+        for m0, y in zip(starts, banks):
+            third_product(0, y, z0_codes[:, m0 : m0 + P], z0_plane[:, m0 : m0 + P])
+        z1_q = [quantize(grouped, "zq1%d" % piece, (0, P)) for piece, grouped in enumerate(z1_grouped)]
+        out_rows = out.rearrange("(c p) m -> p c m", p=P)
+        for m0, y, (codes, plane) in zip(starts, banks, z1_q):
+            third_product(1, y, codes[:], plane[:])
+            weighted = ring.tile([P, chunks, P], F32, name="weighted", bufs=4)
+            score = ring.tile([P, chunks, P], F32, name="score", bufs=4)
+            nc.vector.tensor_tensor(weighted[:], y[:], load_sb[:, :, m0 : m0 + P], ALU.mult)
+            for c in range(chunks):
+                nc.scalar.activation(score[:, c, :], weighted[:, c, :], ACT.Identity, bias=bias_sb[:, c : c + 1])
+            nc.sync.dma_start(out=out_rows[:, :, m0 : m0 + P], in_=score[:])

from contextlib import ExitStack

import concourse.mybir as mybir

K, T, S, PAIRS, H, N = 1024, 4096, 1024, 512, 1024, 512
FLOPS = 2 * (2 * K * H * S + H * N * PAIRS)

F32 = mybir.dt.float32
BF16 = mybir.dt.bfloat16
I32 = mybir.dt.int32
U32 = mybir.dt.uint32
U16 = mybir.dt.uint16
U8 = mybir.dt.uint8
FP8X4 = mybir.dt.float8_e4m3fn_x4
FP4X4 = mybir.dt.float4_e2m1fn_x4
ALU = mybir.AluOpType
ACT = mybir.ActivationFunctionType

P = 128
PACK = 4
PASS = P * PACK
BANK = 512
ROW_TILES = H // P
LAST = ROW_TILES - 1
HALF = PASS // 2
RUN = 4
ROUND_AFTER = 2


def tile_list_electrolyser_pair_minimum_kernel(
    tc, tab_words, tab_scales, offs, w1, w2_words, w2_scales, pos1, pos2, gain, w4_words, w4_scales, bias, load, out
):
    nc = tc.nc
    with ExitStack() as ctx:
        held = ctx.enter_context(tc.tile_pool(name="held", bufs=1))
        big = ctx.enter_context(tc.tile_pool(name="big", bufs=1))
        ring = ctx.enter_context(tc.tile_pool(name="ring", bufs=2))
        psum = ctx.enter_context(tc.psum_pool(name="psum", bufs=4))

        offs_sb = held.tile([P, S // 16], U16, name="offs_sb")
        pos1_sb = held.tile([P, PAIRS // 16], U16, name="pos1_sb")
        pos2_sb = held.tile([P, PAIRS // 16], U16, name="pos2_sb")

        tab_bytes = big.tile([P, T], U8, name="tab_bytes", tag="tab_bytes", align_bytes=64)
        w2_bytes = big.tile([P, H], U8, name="w2_bytes", tag="w2_bytes", align_bytes=64)
        planes = [held.tile([P, S + H], U8, name="planes%d" % kp, align_bytes=64) for kp in range(2)]

        warm = held.tile([P, 2], F32, name="warm")
        nc.vector.memset(warm[:, 0:1], 1.0)
        nc.scalar.activation(warm[:, 1:2], warm[:, 0:1], ACT.Abs_reciprocal_sqrt)
        one = warm[:, 1:2]

        def load_scale_rows(dst, scales):
            nc.sync.dma_start(out=dst.bitcast(I32), in_=scales.rearrange("kp u c -> (kp u) c").bitcast(I32))

        def load_table(kp):
            words = big.tile([P, T], U16, name="tab_w", tag="tab%d" % kp, align_bytes=64)
            nc.sync.dma_start(out=words[:].bitcast(I32), in_=tab_words[kp].bitcast(I32))
            return words

        def load_w1(g, kp, c0, c1, tag):
            raw = big.tile([P, PACK, c1 - c0], F32, name="w1_raw", tag=tag, align_bytes=64)
            rows = w1[kp * PASS : (kp + 1) * PASS, g * PASS + c0 : g * PASS + c1]
            nc.sync.dma_start(out=raw[:], in_=rows.rearrange("(p j) c -> p j c", j=PACK))
            return raw

        def load_w2(g):
            raw = big.tile([P, 2, PASS], I32, name="w2_raw", tag="w2raw", align_bytes=64)
            src = w2_words[:, :, g * PASS : (g + 1) * PASS, :].rearrange("kp p c j -> p kp (c j)")
            nc.sync.dma_start(out=raw[:], in_=src.bitcast(I32))
            return raw

        def round_w1(copy, grouped, raw, c0, c1):
            dst = grouped.rearrange("p (t m j) -> p m j t", t=PACK, j=PACK)[:, c0 // PACK : c1 // PACK]
            copy(out=dst, in_=raw.rearrange("p j (m t) -> p m j t", t=PACK))

        def quantize(grouped, name, cuts):
            codes = big.tile([P, cuts[-1]], U32, name="codes", tag=name, align_bytes=64)
            plane = held.tile([P, cuts[-1]], U8, name=name + "_plane", align_bytes=64)
            for c0, c1 in zip(cuts, cuts[1:]):
                nc.vector.quantize_mx(
                    out=codes[:, c0:c1].bitcast(FP8X4), scales=plane[:, c0:c1], in_=grouped[:, c0 * PACK : c1 * PACK]
                )
            return codes, plane

        v_words, w1_q, w2_q = {}, {}, {}

        def deal_w2_words(g, raw, t0, t1, tag):
            dealt = big.tile([P, 2, (t1 - t0) * P], I32, name="w2_dealt", tag=tag, align_bytes=64)
            nc.vector.tensor_copy(
                out=dealt[:].rearrange("p kp (t c e) -> p kp c t e", t=t1 - t0, e=RUN),
                in_=raw[:].rearrange("p kp (c e t) -> p kp c t e", t=PACK, e=RUN)[:, :, :, t0:t1, :],
            )
            for t in range(t0, t1):
                cols = slice(S + g * PASS + t * P, S + g * PASS + (t + 1) * P)
                words = dealt[:, :, (t - t0) * P : (t - t0 + 1) * P]
                w2_q[g * PACK + t] = [(words[:, kp, :], planes[kp][:, cols]) for kp in range(2)]

        def gather_table(words, kp, half):
            cols = offs_sb[:, half * BANK // 16 : (half + 1) * BANK // 16]
            v_words[kp, half] = held.tile([P, BANK], U16, name="v_words%d%d" % (kp, half), align_bytes=64)
            nc.vector.tensor_copy(out=v_words[kp, half][:], in_=words[:].indirect(cols))

        def first_product(tag, operands, passes):
            sums = [psum.tile([P, BANK], F32, name="acc", tag=tag) for half in range(2)]
            for kp in passes:
                codes, plane = operands[kp]
                for half in range(2):
                    nc.tensor.matmul_mx(
                        out=sums[half][:],
                        lhsT=codes.bitcast(FP8X4),
                        lhsT_scale=plane,
                        rhs=v_words[kp, half][:].bitcast(FP4X4),
                        rhs_scale=planes[kp][:, half * BANK : (half + 1) * BANK],
                        start=(kp == passes[0]),
                        stop=(kp == passes[1]),
                    )
            return sums

        damp_all = held.tile([P, (ROW_TILES + 1) * S], F32, name="damp_all")
        root_tags = {ROUND_AFTER: "root_then_w1", LAST: "root_then_z"}

        def damping(i, spans):
            size = ring.tile([P, S], F32, name="size")
            if i in root_tags:
                root = big.tile([P, S], F32, name="root", tag=root_tags[i], align_bytes=64)
            else:
                root = ring.tile([P, S], F32, name="root")
            damp = damp_all[:, i * S : (i + 1) * S]
            b_sums = first_product("b", w2_q[i], (0, 1))
            for span in spans:
                for half in span:
                    nc.scalar.activation(size[:, half * BANK : (half + 1) * BANK], b_sums[half][:], ACT.Abs)
                cols = slice(span[0] * BANK, (span[-1] + 1) * BANK)
                nc.scalar.activation(root[:, cols], size[:, cols], ACT.Abs_reciprocal_sqrt, bias=one)
                nc.scalar.activation(damp[:, cols], root[:, cols], ACT.Square)

        def features(i):
            g, t = divmod(i, PACK)
            h = ring.tile([P, S], F32, name="h")
            operands = [(codes[:, t * P : (t + 1) * P], plane[:, t * P : (t + 1) * P]) for codes, plane in w1_q[g]]
            a_sums = first_product("a", operands, (1 - g, g))
            for half in range(2):
                c0, c1 = half * BANK, (half + 1) * BANK
                nc.vector.tensor_tensor(h[:, c0:c1], a_sums[half][:], damp_all[:, i * S + c0 : i * S + c1], ALU.mult)
            return h

        def pick(h, pos_sb, name, m0, m1):
            picked = ring.tile([P, m1 - m0], F32, name="picked", tag=name, bufs=4)
            nc.vector.tensor_copy(out=picked[:], in_=h[:].indirect(pos_sb[:, m0 // 16 : m1 // 16]))
            return picked

        def lower(i, inlet, outlet, m0, m1):
            nc.vector.scalar_tensor_tensor(
                out=damp_all[:, (i + 1) * S + m0 : (i + 1) * S + m1],
                in0=outlet[:],
                scalar=gain_sb[:, i : i + 1],
                in1=inlet[:],
                op0=ALU.mult,
                op1=ALU.min,
            )

        def interleave_z(g, m0, m1, tag):
            grouped = big.tile([P, (m1 - m0) * PACK], BF16, name="grouped", tag=tag, align_bytes=64)
            z_rows = damp_all[:, (g * PACK + 1) * S : (g * PACK + PACK + 1) * S].rearrange("p (t s) -> p t s", t=PACK)
            nc.scalar.copy(
                out=grouped[:].rearrange("p (c e t) -> p c t e", t=PACK, e=RUN),
                in_=z_rows[:, :, m0:m1].rearrange("p t (c e) -> p c t e", e=RUN),
            )
            return grouped

        nc.sync.dma_start(offs_sb[:], offs)
        load_scale_rows(tab_bytes[0:32, :], tab_scales)
        load_scale_rows(w2_bytes[0:32, :], w2_scales)
        for rows in (slice(32, 64), slice(64, 128)):
            nc.vector.memset(tab_bytes[rows, :].bitcast(I32), 0)
            nc.gpsimd.memset(w2_bytes[rows, :].bitcast(I32), 0)
        nc.gpsimd.memset(planes[1][:].bitcast(I32), 0)
        tab0 = load_table(0)
        nc.sync.dma_start(pos1_sb[:], pos1)
        nc.sync.dma_start(pos2_sb[:], pos2)
        w2raw0 = load_w2(0)
        raw00_left = load_w1(0, 0, 0, HALF, "w1raw")
        tab1 = load_table(1)

        v_bytes = big.tile([P, S], U8, name="v_bytes", tag="v_bytes", align_bytes=64)
        nc.vector.tensor_copy(out=v_bytes[:], in_=tab_bytes[:].indirect(offs_sb[:]))
        nc.vector.tensor_copy(
            out=planes[0][:, S : S + H].rearrange("p (g t m) -> p g m t", g=2, t=PACK),
            in_=w2_bytes[:].rearrange("p (g m t) -> p g m t", g=2, t=PACK),
        )
        nc.vector.tensor_copy(out=planes[0][:, 0:S].bitcast(I32), in_=v_bytes[:].bitcast(I32))
        moves = [(kp, q) for kp in range(2) for q in range(1 - kp, 4)]
        for kp, q in moves:
            row = 16 * kp + 4 * q
            queue = nc.gpsimd if (kp, q) == moves[-1] else nc.sync
            queue.dma_start(
                out=planes[kp][32 * q : 32 * q + 4, :].bitcast(I32), in_=planes[0][row : row + 4, :].bitcast(I32)
            )
        raw01 = load_w1(0, 1, 0, PASS, "v_bytes")

        gather_table(tab0, 0, 0)
        gather_table(tab0, 0, 1)
        raw00_right = load_w1(0, 0, HALF, PASS, "tab0")
        grouped00 = big.tile([P, PASS * PACK], BF16, name="grouped00", tag="w1_then_w2", align_bytes=64)
        round_w1(nc.scalar.copy, grouped00[:], raw00_left[:], 0, HALF)
        deal_w2_words(0, w2raw0, 0, 2, "w2_dealt_first")
        gather_table(tab1, 1, 0)
        gather_table(tab1, 1, 1)
        raw10 = load_w1(1, 0, 0, PASS, "tab1")
        damping(0, [(0,), (1,)])
        grouped01 = big.tile([P, PASS * PACK], BF16, name="grouped01", tag="w1_then_gain", align_bytes=64)
        round_w1(nc.vector.tensor_copy, grouped01[:], raw01[:], 0, PASS)
        raw11 = load_w1(1, 1, 0, PASS, "v_bytes")
        round_w1(nc.vector.tensor_copy, grouped00[:], raw00_right[:], HALF, PASS)
        q01 = quantize(grouped01, "w1q01", (0, PASS))
        w1_q[0] = [quantize(grouped00, "w1q00", (0, P, 2 * P, PASS)), q01]
        deal_w2_words(0, w2raw0, 2, PACK, "w1_then_w2")
        gain_sb = big.tile([P, ROW_TILES], F32, name="gain_sb", tag="w1_then_gain", align_bytes=64)
        with nc.allow_non_contiguous_dma("four gains to a partition and group"):
            nc.sync.dma_start(
                out=gain_sb[:].rearrange("p (g t) -> p g t", t=PACK),
                in_=gain.rearrange("(g p t) -> p g t", p=P, t=PACK),
            )
        w2raw1 = load_w2(1)

        picked = None
        for i in range(ROW_TILES):
            if i == ROUND_AFTER:
                grouped1 = big.tile([P, 2 * PASS * PACK], BF16, name="grouped1", tag="root_then_w1", align_bytes=64)
                round_w1(nc.scalar.copy, grouped1[:, : PASS * PACK], raw10[:], 0, PASS)
                round_w1(nc.scalar.copy, grouped1[:, PASS * PACK :], raw11[:, :, :HALF], 0, HALF)
                load_sb = big.tile([P, N // P, PAIRS], F32, name="load_sb", tag="tab1", align_bytes=64)
                nc.sync.dma_start(out=load_sb[:], in_=load.rearrange("(c p) m -> p c m", p=P))
            if i < LAST:
                damping(i + 1, [(0, 1)])
            if i == LAST - 1:
                z_grouped0 = interleave_z(0, 0, PAIRS, "root_then_z")
            h = features(i)
            if i > 0:
                lower(i - 1, picked[0], picked[1], 0, PAIRS)
            if i < LAST:
                picked = (pick(h, pos1_sb, "inlet", 0, PAIRS), pick(h, pos2_sb, "outlet", 0, PAIRS))
            if i == 0:
                deal_w2_words(1, w2raw1, 0, PACK, "w2_dealt_second")
                w4_sb = big.tile([P, 2, N], U16, name="w4_sb", tag="w2raw", align_bytes=64)
                nc.sync.dma_start(out=w4_sb[:].bitcast(I32), in_=w4_words.rearrange("kp p c -> p kp c").bitcast(I32))
                w4_planes = big.tile([P, 2, N], U8, name="w4_planes", tag="tab0", align_bytes=64)
                nc.vector.memset(w4_planes[:].rearrange("p kp c -> p (kp c)").bitcast(I32), 0)
                for q in range(4):
                    nc.sync.dma_start(
                        out=w4_planes[32 * q : 32 * q + 4, :, :].bitcast(I32),
                        in_=w4_scales[:, 4 * q : 4 * q + 4, :].rearrange("kp r c -> r kp c").bitcast(I32),
                    )
            if i == ROUND_AFTER:
                round_w1(nc.vector.tensor_copy, grouped1[:, PASS * PACK :], raw11[:, :, HALF:], HALF, PASS)
                bias_sb = big.tile([P, N // P], F32, name="bias_sb", tag="v_bytes", align_bytes=64)
                with nc.allow_non_contiguous_dma("one bias value to a partition"):
                    nc.sync.dma_start(out=bias_sb[:], in_=bias.rearrange("(c p) -> p c", p=P))
                codes1, plane1 = quantize(grouped1, "w1q1", (0, 2 * PASS))
                w1_q[1] = [
                    (codes1[:, kp * PASS : (kp + 1) * PASS], plane1[:, kp * PASS : (kp + 1) * PASS]) for kp in range(2)
                ]

        starts = list(range(0, PAIRS, P))
        z0_codes, z0_plane = quantize(z_grouped0, "zq0", (0, PAIRS))
        outlet = pick(h, pos2_sb, "outlet", 0, P)
        z1_grouped = []
        for m0 in starts:
            inlet = pick(h, pos1_sb, "inlet", m0, m0 + P)
            next_outlet = pick(h, pos2_sb, "outlet", m0 + P, m0 + 2 * P) if m0 < starts[-1] else None
            lower(LAST, inlet, outlet, m0, m0 + P)
            z1_grouped.append(interleave_z(1, m0, m0 + P, "z_piece%d" % (m0 // P)))
            outlet = next_outlet

        chunks = N // P
        banks = [psum.tile([P, chunks, P], F32, name="y", tag="b") for m0 in starts]

        def third_product(g, y, codes, plane):
            for c in range(chunks):
                nc.tensor.matmul_mx(
                    out=y[:, c, :],
                    lhsT=w4_sb[:, g, c * P : (c + 1) * P].bitcast(FP4X4),
                    lhsT_scale=w4_planes[:, g, c * P : (c + 1) * P],
                    rhs=codes.bitcast(FP8X4),
                    rhs_scale=plane,
                    start=(g == 0 and c == 0),
                    stop=(g == 1 and c == chunks - 1),
                )

        for m0, y in zip(starts, banks):
            third_product(0, y, z0_codes[:, m0 : m0 + P], z0_plane[:, m0 : m0 + P])
        z1_q = [quantize(grouped, "zq1%d" % piece, (0, P)) for piece, grouped in enumerate(z1_grouped)]
        out_rows = out.rearrange("(c p) m -> p c m", p=P)
        for m0, y, (codes, plane) in zip(starts, banks, z1_q):
            third_product(1, y, codes[:], plane[:])
            weighted = ring.tile([P, chunks, P], F32, name="weighted", bufs=4)
            score = ring.tile([P, chunks, P], F32, name="score", bufs=4)
            nc.vector.tensor_tensor(weighted[:], y[:], load_sb[:, :, m0 : m0 + P], ALU.mult)
            for c in range(chunks):
                nc.scalar.activation(score[:, c, :], weighted[:, c, :], ACT.Identity, bias=bias_sb[:, c : c + 1])
            nc.sync.dma_start(out=out_rows[:, :, m0 : m0 + P], in_=score[:])
